import numpy as np, ml_dtypes
CORES = [10,34,74,98]
N = 4
BF = ml_dtypes.bfloat16
W, E, B, C, RO, NC = 2048, 1024, 256, 12, 3, 32
def group(rng, noise, good, mode, proto):
    n = W // NC; mem = rng.permutation(W).reshape(NC, n); cl = np.zeros(W, np.int64); cl[mem] = np.arange(NC)[:, None]
    x = np.minimum(np.maximum(proto[:, cl] + rng.integers(-noise, noise + 1, (16, W)), 0), 63)
    nx = rng.integers(0, NC, (16, NC))
    if mode == 1: nx[:] = np.arange(NC)
    if mode == 2: nx[:] = cl[0]
    if mode == 3: nx[:] = cl[W - 1]
    l = mem[nx[:, cl], rng.integers(0, n, (16, W))]
    if mode == 1: l[:] = np.arange(W)
    if mode == 2: l[:] = 0
    if mode == 3: l[:] = W - 1
    i = np.zeros((16, E), np.int64); q = rng.integers(0, NC, E)
    for k in range(16):
        i[k] = mem[q, rng.integers(0, n, E)]
        if k < 15:
            go = nx[k, q]; q = np.where(good[k], go, (go + rng.integers(1, NC, E)) % NC)
    return x, i, l
def parts(rng, style):
    x = np.zeros((N, 8, 16, W), np.int64); i = np.zeros((N, 8, 16, E), np.int64); l = np.zeros((N, 8, 16, W), np.int64)
    for a in range(N):
        for g in range(8):
            noise = int(rng.integers(1, 4)); mode = 0; proto = rng.integers(0, 64, (16, NC))
            good = rng.random((15, E)) < rng.choice(np.array([0.2, 0.6, 0.8, 0.95, 1.0]), E)
            if style == "ties": noise = 0; proto = 16 + 8 * rng.integers(0, 2, (16, NC))
            if style == "corners":
                noise = 0; mode = (a + g) % 4; n = rng.choice(np.array([0, 1, C - 1, C, C + 1, 15]), E)
                good = np.argsort(np.argsort(rng.random((15, E)), axis=0), axis=0) < n
            x[a, g], i[a, g], l[a, g] = group(rng, noise, good, mode, proto)
    t = np.stack([rng.integers(20, 70, (N, 8, 16)), rng.integers(200, 420, (N, 8, 16))], axis=-1)
    return x, rng.integers(0, 64, (N, 8, 16, E)), i, l, rng.integers(0, 64, (N, 8, 16, B)), rng.integers(0, 256, (N, 8, 16, 1)), rng.integers(0, 2048, (N, 8, 16, 2)), t
def pack(x, gs, i, l, z, w, h, t):
    def bf(v): return np.ascontiguousarray(v.reshape(N, 128, -1)).astype(np.float32).astype(BF)
    def whole(v): return np.ascontiguousarray(v.reshape(N, 128, -1)).astype(np.int32)
    return {"xc": bf(x), "gi": bf(gs), "ix": whole(i), "lk": whole(l), "zc": bf(z), "wt": whole(w), "hk": whole(h), "th": whole(t)}
def ends(rng, lo, hi, shape, share):
    v = np.where(rng.random(shape) < 0.5, lo, hi)
    return np.where(rng.random(shape) < share, v, rng.integers(lo, hi + 1, shape))
def records(rng, n):
    k = rng.integers(0, 3, (N, 8, 1, n))
    return np.where(k == 0, 0, np.where(k == 1, 63, ends(rng, 0, 63, (N, 8, 16, n), 1.0)))
def full(rng, p):
    u = rng.permutation(4096); f, k = np.unique(((u * u >> 5) + p * u) & (E - 1), return_index=True)
    return u[rng.permutation(k)[:B]]
def setup_inputs(rng):
    return pack(*parts(rng, "plain"))
def setup_inputs_ties(rng):
    x, gs, i, l, z, w, h, t = parts(rng, "ties")
    gs = 16 + 8 * rng.integers(0, 2, gs.shape); z = 16 + 8 * rng.integers(0, 2, z.shape)
    t = rng.choice(np.array([56, 63, 64, 65, 72]), t.shape)
    for a in range(N):
        for g in (6, 7):
            v = (256, 257, 259, 513, 515, 767, 1005, 1007)[(a + g) & 7]; base = int(rng.integers(0, 1008 - v))
            m = rng.permutation(W); low = np.flatnonzero(m < W // 2); high = np.flatnonzero(m >= W // 2)
            size = base + np.where(m < W // 2, 0, v + (rng.random(W) < 0.3).astype(np.int64))
            x[a, g] = (size >> 4) + (np.arange(16)[:, None] < (size & 15)).astype(np.int64)
            i[a, g] = low[rng.integers(0, W // 2, (16, E))]; l[a, g] = high[rng.integers(0, W // 2, (16, W))]
            t[a, g, :, 0] = v; t[a, g, :, 1] = 1008
    return pack(x, gs, i, l, z, w, h, t)
def setup_inputs_corners(rng):
    x, gs, i, l, z, w, h, t = parts(rng, "corners")
    for a in range(N):
        for g in range(8):
            kind = (3 * a + g) % 4
            if kind == 0: w[a, g] = 255
            if kind == 1: w[a, g] = 255 * rng.integers(0, 2, (16, 1))
            if kind == 2: w[a, g] = 0; w[a, g, 15] = 1
            t[a, g, :, 0] = (0, 1, 40, 0, 0, 1008, 40, 1)[(a + g) % 8]
            t[a, g, :, 1] = rng.choice(np.array([0, 340, 1008]), 16)
            h[a, g] = np.where(rng.random((16, 2)) < 0.4, 2047 * rng.integers(0, 2, (16, 2)), h[a, g])
    k = rng.integers(0, 4, (N, 8, 1, B)); z = np.where(k == 0, 0, np.where(k == 1, 63, z))
    k = rng.integers(0, 4, (N, 8, 1, E)); gs = np.where(k == 0, 0, np.where(k == 1, 63, gs))
    i = np.where(rng.random((N, 8, 1, E)) < 0.1, (W - 1) * rng.integers(0, 2, (N, 8, 1, E)), i)
    return pack(x, gs, i, l, z, w, h, t)
def setup_inputs_crowd(rng):
    x, gs, i, l, z, w, h, t = parts(rng, "plain")
    w[:, 0::4] = 0; w[:, 0::4, 5] = 1; z[:, 0::4, 5] = rng.integers(0, 6, (N, 2, B)); h[:, 0::4, :, 0] = 0
    i[:, 1] = rng.choice(np.array([0, 1, W // 2, W - 2, W - 1]), (N, 16, E)); gs[:, 1] = 30
    w[:, 2] = 0
    z[:, 3] = z[:, 3][..., rng.integers(0, 3, B)]
    for a in range(N):
        for g in (5, 6, 7):
            w[a, g] = 0; w[a, g, 0] = 1; w[a, g, 1] = 64; gs[a, g] = 0
            p = int(h[a, g, 0, 0]); u = full(rng, p)
            if g == 5: u[B // 2:] = u[:B // 2]
            z[a, g, 0] = u & 63; z[a, g, 1] = u >> 6
            e = ((u * u >> 5) + p * u) & (E - 1)
            if g == 5:
                side = rng.random(B // 2) < 0.5; side[0] = True; side[1] = False; near = np.concatenate([side, ~side])
                x[a, g] = rng.integers(16, 25, (16, W)); i[a, g] = rng.integers(0, W, (16, E))
                z[a, g, 2:] = np.where(near, rng.integers(16, 25, (14, B)), rng.integers(56, 64, (14, B)))
                t[a, g, :, 0] = 0; t[a, g, :, 1] = rng.integers(206, 448, 16)
            if g == 6:
                o = rng.permutation(W); i[a, g][:, e] = o[(np.arange(16)[:, None] % (W // B)) * B + np.arange(B)]
                t[a, g, :, 0] = 0
            if g == 7: t[a, g, :, 0] = 1008
    t[2, :, :, 0] = 0
    gs[2, 3] = 30; c = int(rng.integers(0, W)); u = np.add.reduce(w[2, 3] * z[2, 3], axis=0) & 4095
    e = ((u * u >> 5) + h[2, 3, 0, 0] * u) & (E - 1)
    i[2, 3][:, e] = c; l[2, 3][:, c] = c
    return pack(x, gs, i, l, z, w, h, t)
def setup_inputs_spread(rng):
    x, gs, i, l, z, w, h, t = parts(rng, "plain")
    x = x >> rng.integers(0, 7, (N, 8, 1, W)); gs = gs >> rng.integers(0, 7, (N, 8, 1, E)); z = z >> rng.integers(0, 7, (N, 8, 1, B))
    i[:, ::2] = (W * rng.random((N, 4, 16, E)) ** 3).astype(np.int64); l[:, ::4] = (W * rng.random((N, 2, 16, W)) ** 3).astype(np.int64)
    w = np.exp2(8 * rng.random(w.shape)).astype(np.int64); h = np.exp2(11 * rng.random(h.shape)).astype(np.int64)
    t = np.minimum(np.exp2(10.2 * rng.random(t.shape)).astype(np.int64), 1008)
    return pack(x, gs, i, l, z, np.minimum(w, 255), np.minimum(h, 2047), t)
def setup_inputs_ends(rng):
    x = records(rng, W); gs = records(rng, E); z = records(rng, B)
    x[:, 0::2, :, 0] = 63; x[:, 0::2, :, W - 1] = 0; x[:, 1::2, :, 0] = 0; x[:, 1::2, :, W - 1] = 63
    i = ends(rng, 0, W - 1, (N, 8, 16, E), 0.75); l = ends(rng, 0, W - 1, (N, 8, 16, W), 0.75)
    w = ends(rng, 0, 255, (N, 8, 16, 1), 0.75); w[:, 7] = 255
    h = ends(rng, 0, 2047, (N, 8, 16, 2), 0.8); t = ends(rng, 0, 1008, (N, 8, 16, 2), 1.0)
    t[0, :, :, 0] = 1008; a = N - 1; t[a, 7, :, 0] = 0
    i[0, 5] = W - 1; l[0, 5, :, W - 1] = 0
    t[1, :, :, 0] = 1008; t[1, 6, :, 0] = 0
    w[1, 6] = 0; w[1, 6, 15] = 255; z[1, 6, 15] = 0; z[1, 6, 15, B - 1] = 63; h[1, 6, :, 0] = 2047 * rng.integers(0, 2, 16)
    i[1, 6] = W - 1; i[1, 6, :, 0] = 0; l[1, 6, :, 0] = 0; l[1, 6, :, W - 1] = 0
    v = z[a, 7]; v[:, B - 1] = 63; v[:, B - 2] = 0; v[15, B - 2] = 63; v[:, B - 3] = 0; v[:4, B - 3] = 63; v[4, B - 3] = 5
    h[a, 7, 0, 0] = 2047; h[a, 7, 1, 0] = 0; h[a, 7, 15, 1] = 2047
    h[a, 7, 15, 0] = ((E - 1 - (3777 * 3777 >> 5)) * pow(3777, -1, E)) % E
    c = ((3088 * 3088 >> 5) + h[a, 7, :, 0] * 3088) & (E - 1)
    gs[a, 7][:, c] = 0; gs[a, 7, :, E - 1] = v[:, B - 2]
    i[a, 7, :, c[1]] = 0; i[a, 7, :, c[0]] = W - 1; i[a, 7, :8, E - 1] = 0; i[a, 7, 8:, E - 1] = W - 1
    l[a, 7, :, 0] = 0; l[a, 7, :, W - 1] = 0
    return pack(x, gs, i, l, z, w, h, t)
def check_inputs(d):
    bad = []
    for k, lo, hi in (("xc", 0, 63), ("gi", 0, 63), ("ix", 0, W - 1), ("lk", 0, W - 1), ("zc", 0, 63), ("wt", 0, 255), ("hk", 0, 2047), ("th", 0, 1008)):
        v = np.asarray(d[k]).astype(np.float64)
        if not np.all((v >= lo) & (v <= hi) & (v == np.floor(v))): bad.append("range of " + k)
    return bad
def reference(xc, gi, ix, lk, zc, wt, hk, th):
    def cut(v): return np.asarray(v).astype(np.float32).astype(np.int64).reshape(N, 8, 16, -1)
    X, G, I, L, Z, w, h, t = cut(xc), cut(gi), cut(ix), cut(lk), cut(zc), cut(wt), cut(hk), cut(th)
    A = np.zeros(N, np.int64); lane = np.arange(B)
    for rnd in range(RO):
        count = np.zeros(N, np.int64)
        for a in range(N):
            r = (a - rnd) % N
            for g in range(8):
                z = Z[r, g]
                u = np.add.reduce(w[a, g] * z, axis=0) & 4095
                em = ((u * u >> 5) + h[a, g, :, 0:1] * u + A[a]) & (E - 1)
                d = np.add.reduce(np.abs(G[a, g][:, em] - z[:, None, :]), axis=0)
                e = em[np.argmin(d, axis=0), lane]
                J = I[a, g][:, e]
                x = X[a, g][:, J]
                y = X[a, g][:, np.take_along_axis(L[a, g], J, 1)]
                s = np.add.reduce(np.abs(y[:, :15] - x[:, 1:]), axis=0)
                far = np.add.reduce(np.abs(x - z[:, None, :]), axis=0)
                rec = np.add.reduce((s <= t[a, g, :15, 0:1]).astype(np.int64), axis=0) >= C
                fresh = ((u * u >> 4) + h[a, g, :, 1:2] * u) & (W - 1)
                col = np.where(rec[None, :] | (far > t[a, g, :, 1:2]), fresh, J)
                ks = np.argmax(s, axis=0)
                f, first = np.unique(e, return_index=True)
                I[a, g][:, f] = col[:, first]
                if rnd < RO - 1:
                    o = first[rec[first]]; G[a, g][:, e[o]] = z[:, o]
                q = np.flatnonzero(~rec); c, one = np.unique(J[ks[q], q], return_index=True); q = q[one]
                L[a, g][ks[q], c] = J[ks[q] + 1, q]
                count[a] += np.count_nonzero(rec)
                Z[r, g] = (z + np.maximum.reduce(x, axis=1)) >> 1
        A = count
    return {"yz": Z.reshape(N, 128, B).astype(np.float32).astype(BF), "yi": I.reshape(N, 128, E).astype(np.float32), "yl": L.reshape(N, 128, W).astype(np.float32)}

@@ -1,0 +1,640 @@
+import numpy as np
+from concourse.mybir import AluOpType as A, AxisListType, ActivationFunctionType as F
+
+BIG = 1.0e9
+OFF24 = 16777216.0
+CYC = 0.8333
+GAT, SCA, WAKE, FIX = 1.56, 3.8, 70.0, 20.0
+SCRATCH, SIZES = {}, {}
+TWO = ("bfloat16", "float16", "uint16")
+
+
+def _buf(name, cols, dtype, where="sbuf"):
+    SCRATCH[name] = (where, [128, cols], dtype)
+
+
+for _n, _c, _d in (
+        ("xb", 2048, "bfloat16"), ("G", 1280, "bfloat16"), ("ixi", 1024, "int32"), ("I", 1280, "float32"),
+        ("lki", 2048, "int32"), ("L", 2304, "float32"),
+        ("wti", 1, "int32"), ("hki", 2, "int32"), ("thi", 2, "int32"),
+        ("z0", 256, "bfloat16"), ("z1", 256, "bfloat16"), ("z2", 256, "bfloat16"), ("z3", 256, "bfloat16"),
+        ("zs0", 256, "bfloat16"), ("zs1", 256, "bfloat16"), ("zs2", 256, "bfloat16"), ("zt", 256, "bfloat16"),
+        ("pI", 1, "int32"), ("p16i", 1, "int32"), ("pgi", 1, "int32"), ("pf", 1, "float32"), ("p16", 1, "float32"),
+        ("pg", 1, "float32"), ("pz", 1, "float32"), ("colA", 1, "float32"), ("colB", 1, "float32"), ("k15", 1, "float32"),
+        ("wf", 1, "float32"), ("hf", 2, "float32"), ("tf", 2, "float32"),
+        ("dI", 144, "int32"), ("cI", 144, "int32"), ("gI", 128, "int32"), ("g8I", 16, "int32"), ("rI", 256, "int32"),
+        ("dgI", 128, "int32"), ("duI", 16, "int32"), ("r15I", 256, "int32"),
+        ("IW", 136, "float16"), ("IB", 136, "bfloat16"), ("INB", 136, "bfloat16"), ("BB", 128, "bfloat16"), ("BH", 128, "float16"),
+        ("BLK", 16, "bfloat16"), ("Q16", 8, "float16"), ("MK", 256, "float16"), ("ZB", 144, "bfloat16"),
+        ("SEL", 2048, "float16"), ("KM", 16, "float32"), ("CD", 128, "bfloat16"), ("CS", 256, "bfloat16"),
+        ("ONB", 128, "bfloat16"), ("ONH", 128, "float16"), ("MMIN", 128, "float32"), ("MMAX", 256, "float32"),
+        ("MR", 2048, "bfloat16"), ("OFFR", 8, "uint16"), ("pk1", 1, "float32"), ("pk2", 1, "float32"), ("pk3", 1, "float32"),
+        ("PICK", 2, "uint16"), ("DUE", 16, "float32"), ("DUJ", 16, "float32"), ("DM", 2176, "bfloat16"), ("OWN", 16, "bfloat16"),
+        ("RPR", 128, "float16"), ("RPJ", 128, "float16"), ("RPt", 128, "float16"), ("RPN", 128, "float16"), ("RPK", 128, "float16"),
+        ("dgA", 128, "float16"), ("THR", 128, "float32"), ("Wb", 128, "bfloat16"),
+        ("W8", 8, "bfloat16"), ("ZQ", 200, "float16"), ("PM_0", 128, "float16"), ("PM_1", 128, "float16"), ("PQ_0", 128, "float16"), ("PQ_1", 128, "float16"),
+        ("C0", 256, "bfloat16"), ("BL2", 16, "bfloat16"), ("BLN", 16, "bfloat16"), ("CDi", 128, "bfloat16"), ("CSi", 256, "bfloat16"),
+        ("ui", 16, "int32"), ("uu", 16, "int32"), ("UQ", 48, "int32"), ("UH", 48, "float16"), ("RLu", 128, "float16"), ("em", 256, "int32"), ("emu", 256, "uint16"), ("emh", 256, "float16"),
+        ("sh4", 256, "int32"), ("vi", 256, "int32"), ("vJ", 256, "float32"), ("Jf", 256, "float32"), ("Jh", 256, "float16"),
+        ("zx", 4096, "bfloat16"), ("e_rq", 16, "float32"), ("Y", 256, "float16"), ("Er", 256, "float16"),
+        ("far", 256, "float32"), ("ch", 256, "float32"), ("tmp", 256, "float32"), ("RL", 256, "float16"), ("RJh", 256, "float16"),
+        ("mj", 256, "float32"), ("scj", 256, "float32"), ("EQE", 2176, "bfloat16"), ("DUPE", 2176, "bfloat16"),
+        ("EQJ", 2176, "bfloat16"), ("DUPJ", 2176, "bfloat16"), ("fl", 16, "float32"), ("of1", 16, "float32"), ("of2", 16, "float32"),
+        ("nr", 16, "float32"), ("og1", 16, "float32"), ("og2", 16, "float32"), ("flJ", 16, "float32"), ("oj1", 16, "float32"),
+        ("oj2", 16, "float32"), ("oj3", 16, "float32"), ("oEu", 16, "uint16"), ("oGu", 16, "uint16"), ("oJu", 16, "uint16"),
+        ("Lold", 256, "float32"), ("mk", 256, "float32"), ("t1", 256, "float32"), ("t2", 256, "float32"), ("Ac", 1, "float32")):
+    _buf(_n, _c, _d)
+for _h in "01":
+    for _n, _c, _d in (("DG", 2048, "bfloat16"), ("AG", 2048, "bfloat16"), ("x", 2064, "bfloat16"), ("Lg", 2048, "float16"), ("mx", 2048, "bfloat16"),
+                       ("Dy", 2048, "bfloat16"), ("Ay", 2048, "bfloat16"), ("Af", 2048, "bfloat16"), ("km", 128, "float32"),
+                       ("ei", 8, "int32"), ("ej", 8, "int32"), ("ME", 128, "float16"), ("eu", 8, "uint16"), ("Ju", 128, "uint16"), ("nu", 128, "uint16"),
+                       ("le", 128, "bfloat16"), ("cs", 128, "bfloat16"), ("sm", 256, "float32"), ("si", 16, "int32"), ("sj", 24, "int32"), ("QT", 32, "float16")):
+        _buf(_n + "_" + _h, _c, _d)
+for _b in range(8):
+    _buf("b%d" % _b, 512, "float32", "psum")
+PLACE = {}
+_pack = {}
+for _n in sorted(SCRATCH):
+    _w, _s, _d = SCRATCH[_n]
+    if _w == "sbuf" and _n not in ("xb", "G", "I", "L", "ixi", "lki", "z0", "z1", "z2", "z3", "zs0", "zs1", "zs2") and _s[1] < 2000:
+        _o = _pack.get(_d, 0)
+        PLACE[_n] = ("k_" + _d, _o)
+        _pack[_d] = _o + (_s[1] + 31) // 32 * 32
+    else:
+        PLACE[_n] = (_n, 0)
+DTYPE = {_n: SCRATCH[_n][2] for _n in SCRATCH}
+for _n in list(SCRATCH):
+    if PLACE[_n][0] != _n:
+        del SCRATCH[_n]
+for _d in _pack:
+    _buf("k_" + _d, _pack[_d], _d)
+SEMAPHORES = ["qv", "qs", "qt", "qg", "loc", "arr1", "arr2", "arr3"] + ["d%d" % i for i in range(16)]
+
+
+def R(buf, a=0, b=None, step=1, p=128):
+    if b is None:
+        b = a + 1
+    return (buf, a, b, step, p)
+
+
+def width(r):
+    return (r[2] - r[1] + r[3] - 1) // r[3]
+
+
+def clash(r, s):
+    if r[0] != s[0] or r[1] >= s[2] or s[1] >= r[2]:
+        return False
+    return not (r[3] == s[3] and r[3] > 1 and (r[1] - s[1]) % r[3] != 0)
+
+
+class IndOp(tuple):
+    pass
+
+
+def ind(win, off):
+    return IndOp((win, off))
+
+
+def build(rank, opt):
+    ops, loaded = [], [0.0]
+
+    def add(q, kind, calls, reads, writes, cost, lat=0.0, **kw):
+        ops.append(dict(q=q, kind=kind, calls=calls, reads=reads, writes=writes, cost=cost, lat=lat, i=len(ops), **kw))
+
+    def flat(x):
+        if isinstance(x, IndOp):
+            return [x[0], x[1]]
+        return [x] if isinstance(x, tuple) else []
+
+    def small(rs):
+        return all(DTYPE[r[0]] in TWO for r in rs)
+
+    def price(n, half=False, mult=1.0):
+        return max(64.0, n * (0.5 if half else 1.0) * mult) * CYC + FIX
+
+    def V(name, out, *args):
+        full = [x for x in args if isinstance(x, tuple)]
+        rd = [y for x in full for y in flat(x)]
+        wr = flat(out)[:1]
+        if isinstance(out, IndOp):
+            rd = rd + [out[1]]
+            n = width(out[1]) * 16
+            c = 50 + n * SCA * CYC
+        elif any(isinstance(x, IndOp) for x in full):
+            c = 50 + width(out) * GAT * CYC
+        elif name == "tensor_tensor":
+            ps = any(x[0][0] == "b" and len(x[0]) == 2 for x in full)
+            c = price(width(out), False, 1.0 if ps else 2.0)
+        elif name == "tensor_reduce":
+            c = price(width(args[0]))
+        else:
+            c = price(width(out), small([out] + [x for x in full if width(x) > 1]))
+        add("v", name, [(out,) + args], rd, wr, c)
+
+    def VM(name, items):
+        if not items:
+            return
+        n0 = len(ops)
+        for it in items:
+            V(name, *it)
+        got = ops[n0:]
+        del ops[n0:]
+        add("v", name, [o["calls"][0] for o in got], [r for o in got for r in o["reads"]], [r for o in got for r in o["writes"]], sum(o["cost"] for o in got))
+
+    def S(out, in_, func, bias=None, scale=None):
+        c = (65 + width(out) * GAT * CYC) if isinstance(in_, IndOp) else width(out) * CYC + 60
+        rd = flat(in_) + [x for x in (bias, scale) if isinstance(x, tuple)]
+        add("s", "activation", [(out, in_, func, bias, scale)], rd, [out], c)
+
+    def P(items):
+        c = 0.0
+        for o, l, r, a, b in items:
+            f32 = DTYPE[l[0]] == "float32"
+            c += max(min(64, width(l)), width(r)) * (4 if f32 else 1) * CYC + 5
+        rd, wr = [], []
+        for o, l, r, a, b in items:
+            for x in (l, r):
+                if x not in rd:
+                    rd.append(x)
+            if o not in wr:
+                wr.append(o)
+        add("t", "matmul", items, rd, wr, c)
+
+    def iota(out, pattern, base, cm):
+        add("g", "iota", [(out, pattern, base, cm)], [], [out], 130 + 2 * width(out) * CYC)
+
+    def dma(q, out, in_, nbytes, sem):
+        rd = [in_] if isinstance(in_, tuple) else []
+        wr = [out] if isinstance(out, tuple) else []
+        loaded[0] += nbytes * 128 / 200.0 if wr else 0.0
+        add(q, "dma", [(out, in_)], rd, wr, 60, 2000 + (loaded[0] if wr else nbytes * 128 / 200.0), sem=sem)
+
+    dma("y", R("z0", 0, 256), "zc", 512, "d0")
+    dma("s", R("wti", 0, 1), "wt", 4, "d1")
+    dma("s", R("hki", 0, 2), "hk", 8, "d2")
+    dma("y", R("G", 0, 1024), "gi", 2048, "d3")
+    dma("y", R("ixi", 0, 1024), "ix", 4096, "d4")
+    dma("y", R("xb", 0, 2048), "xc", 4096, "d5")
+    dma("s", R("thi", 0, 2), "th", 8, "d6")
+    dma("y", R("lki", 0, 2048), "lk", 8192, "d7")
+    iota(R("pI", 0, 1), [[0, 1]], 0, 1)
+    iota(R("gI", 0, 128), [[1, 8], [0, 16]], 0, 0)
+    iota(R("dI", 0, 144), [[1, 144]], 0, -1)
+    iota(R("g8I", 0, 16), [[0, 2], [1, 8]], 0, 0)
+    iota(R("rI", 0, 256), [[0, 16], [1, 16]], 0, 0)
+    iota(R("cI", 0, 144), [[1, 144]], 0, 0)
+    iota(R("r15I", 0, 256), [[0, 16], [-1, 16]], 15, 0)
+    iota(R("duI", 0, 16), [[16, 16]], 0, 0)
+    iota(R("dgI", 0, 128), [[1, 8], [0, 16]], 0, -1)
+    c1 = lambda b: R(b, 0, 1)
+    ts, tt, tc = "tensor_scalar", "tensor_tensor", "tensor_copy"
+    V(ts, c1("pgi"), c1("pI"), 4, None, A.arith_shift_right)
+    V(tc, c1("pg"), c1("pgi"))
+    V(tc, c1("wf"), c1("wti"))
+    V(ts, R("W8", 0, 8), R("g8I", 0, 8), c1("pg"), c1("wf"), A.is_equal, A.mult)
+    V(tc, R("hf", 0, 2), R("hki", 0, 2))
+    V("memset", R("ZQ", 0, 200), 0.0)
+    V(ts, R("ZQ", 48, 56), R("g8I", 0, 8), c1("pg"), None, A.is_equal)
+    V(ts, R("ZQ", 152, 160), R("g8I", 0, 8), c1("pg"), 0.0625, A.is_equal, A.mult)
+    V(ts, R("BH", 0, 128), R("gI", 0, 128), c1("pg"), None, A.is_equal)
+    V(ts, c1("p16i"), c1("pI"), 15, None, A.bitwise_and)
+    V(tc, c1("p16"), c1("p16i"))
+    V(tc, c1("pf"), c1("pI"))
+    V(ts, R("IW", 0, 136), R("dI", 0, 136), 4.0, None, A.is_equal)
+    V(ts, R("BLK", 0, 16), R("g8I", 0, 16), c1("pg"), 32768.0, A.is_equal, A.mult)
+    V(ts, R("Q16", 0, 8), R("g8I", 0, 8), c1("pg"), None, A.is_equal)
+    V(ts, R("MK", 0, 256), R("rI", 0, 256), c1("p16"), None, A.is_equal)
+    V(tc, R("OFFR", 0, 8), R("g8I", 0, 8))
+    V(ts, c1("colA"), c1("pf"), 64.0, 32.0, A.is_ge, A.mult)
+    V(ts, c1("colB"), c1("pf"), 64.0, -262144.0, A.is_lt, A.mult)
+    V("memset", R("ONB", 0, 128), 1.0)
+    V(ts, R("CD", 0, 128), R("rI", 0, 128), c1("colA"), c1("colB"), A.mult, A.add)
+    V(ts, R("mj", 0, 256), R("rI", 0, 256), 0.0, 2 * BIG, A.is_equal, A.mult)
+    V(ts, R("MMIN", 0, 128), R("mj", 0, 128), -BIG, None, A.add)
+    V("memset", c1("pz"), 0.0)
+
+    def factors(j, name, at):
+        V(ts, R("dgA", 0, 128), R("IW", 4, 132), R("hf", j, j + 1), None, A.mult)
+        for h in (0, 1):
+            o = R("b4", 128 + 128 * h, 256 + 128 * h, 1, 48)
+            P([(o, R("ZQ", 48 - 8 * h, 96 - 8 * h), R("dgA", 0, 128), True, False), (o, R("ZQ", at - 8 * h, at + 48 - 8 * h), R("BH", 0, 128), False, True)])
+            S(R(name + str(h), 0, 128, 1, 48), o, F.Copy)
+    factors(0, "PM_", 120)
+    if any(opt["rg"]):
+        V("memset", R("C0", 0, 256), -131072.0)
+        V(ts, R("BL2", 0, 16), R("BLK", 0, 16), 2.0, None, A.mult)
+        V(ts, R("BLN", 0, 16), R("BLK", 0, 16), -1.0, None, A.mult)
+        V(ts, R("CDi", 0, 128), R("rI", 0, 128), c1("colA"), None, A.mult)
+
+    def load_names():
+        V(tc, R("I", 0, 1024), R("ixi", 0, 1024))
+
+    def load_links():
+        V("memset", R("L", 2048, 2304), 0.0)
+        S(R("L", 0, 1024), R("lki", 0, 1024), F.Copy)
+        S(R("L", 1024, 2048), R("lki", 1024, 2048), F.Copy)
+
+    def late_constants():
+        V(ts, R("IB", 0, 136), R("dI", 0, 136), 4.0, None, A.is_equal)
+        V(ts, R("INB", 0, 136), R("dI", 0, 136), 4.0, -1.0, A.is_equal, A.mult)
+        V(ts, R("KM", 0, 16), R("rI", 0, 16), c1("p16"), None, A.is_equal)
+        for k in range(16):
+            S(R("SEL", 128 * k, 128 * k + 128), R("IW", 4, 132), F.Copy, None, R("KM", k, k + 1))
+        V("memset", R("MR", 0, 2048), 1.0)
+        V("memset", R("MR", 0, 2048, 16), 0.0)
+        V("memset", R("x_0", 2048, 2064), 0.0)
+        V("memset", R("x_1", 2048, 2064), 0.0)
+        V(ts, c1("pk3"), c1("pg"), 16.0, 15.0, A.mult, A.add)
+        V(ts, R("ZB", 0, 144), R("cI", 0, 144), c1("pk3"), None, A.is_equal)
+        V(ts, R("CS", 0, 256), R("r15I", 0, 256), c1("colA"), c1("colB"), A.mult, A.add)
+        V(ts, R("MMAX", 0, 256), R("mj", 0, 256), -1.0, BIG, A.mult, A.add)
+        V(tc, R("tf", 0, 2), R("thi", 0, 2))
+        V("memset", R("ONH", 0, 128), 1.0)
+        V(ts, R("dgA", 0, 128), R("IW", 4, 132), R("tf", 0, 1), None, A.mult)
+        P([(R("b4", 0, 128), R("ONH", 0, 128), R("dgA", 0, 128), True, True)])
+        V(ts, R("THR", 0, 128), R("b4", 0, 128), 32768.0, 32768.0 - OFF24, A.mult, A.add)
+        V("memset", R("THR", 15, 128, 16), -2.0e7)
+        factors(1, "PQ_", 136)
+        if not any(opt["rg"]):
+            V("memset", R("C0", 0, 256), -131072.0)
+            V(ts, R("BL2", 0, 16), R("BLK", 0, 16), 2.0, None, A.mult)
+            V(ts, R("BLN", 0, 16), R("BLK", 0, 16), -1.0, None, A.mult)
+        V(ts, R("CSi", 0, 256), R("r15I", 0, 256), c1("colA"), None, A.mult)
+        V(ts, c1("pk1"), c1("p16"), 8.0, 24.0, A.mult, A.add)
+        V(tt, c1("pk2"), c1("pk1"), c1("p16"), A.mult)
+        V(ts, R("PICK", 0, 1), c1("pk2"), 15.0, None, A.add)
+        V(ts, R("DUE", 0, 16), R("duI", 0, 16), c1("p16"), 1024.0, A.add, A.add)
+        V(ts, R("DUJ", 0, 16), R("duI", 0, 16), c1("p16"), 2048.0, A.add, A.add)
+        V("memset", R("DM", 0, 2176), 1.0)
+        V(ts, R("OWN", 0, 16), R("rI", 0, 16), c1("p16"), 1.0, A.is_equal, A.add)
+        for q in range(16):
+            e = 8 * (q + 1) * (q + 2)
+            S(R("DM", e - 16, e), R("OWN", 0, 16), F.Copy)
+        for q in range(16):
+            s = 8 * q * (q + 1)
+            S(R("DM", s, s + 1), c1("pz"), F.Copy)
+        V(ts, c1("k15"), c1("p16"), -1.0, 15.0, A.mult, A.add)
+        V(ts, R("RPR", 0, 128), R("dgI", 0, 128), 0.0, None, A.is_equal)
+        V(ts, R("RPt", 0, 128), R("dgI", 0, 128), 0.0, 4096.0, A.is_equal, A.mult)
+        V(ts, R("RPJ", 0, 128), R("dgI", 0, 128), -8.0, None, A.is_equal)
+        V(tt, R("RPJ", 0, 128), R("RPJ", 0, 128), R("RPt", 0, 128), A.add)
+        V(ts, R("RPN", 0, 128), R("dgI", 0, 128), -16.0, None, A.is_equal)
+        V(ts, R("RPK", 0, 128), R("dgI", 0, 128), -24.0, None, A.is_equal)
+
+    def dedupe(row, col, cw, eq, du, fl):
+        items = []
+        for q in range(16):
+            s, n = 8 * q * (q + 1), 16 * (q + 1)
+            items.append((R(eq, s, s + n), R(row, 0, n), cw(q), None, A.is_equal))
+        for a in range(0, 16, 4):
+            VM(ts, items[a:a + 4])
+        V("tensor_tensor_scan", R(du, 0, 2176), R("DM", 0, 2176), R(eq, 0, 2176), 0.0, A.mult, A.max)
+        V(ts, R(fl, 0, 16), ind(R(du, 0, 2176), R("PICK", 0, 1)), -1.0, None, A.add)
+
+    def size(relu, out, in_):
+        if relu:
+            V(ts, out, in_, 0.0, None, A.max)
+        else:
+            S(out, in_, F.Abs)
+
+    def keys(relu, K, n, m, d, a, con, coni, payload):
+        if relu:
+            P([(R(K, 0, n), R("ONB", 0, 128), R("C0", 0, n), True, False)] +
+              [(R(K, k, n, 16), R(d, k, 2048, 16), R("BLN", 0, n // 16), False, False) for k in range(m)])
+            P([(R(K, k, n, 16), R(a, k, 2048, 16), R("BL2", 0, n // 16), False, False) for k in range(m)] +
+              [(R(K, 0, n), R("ONB", 0, 128), R(coni, 0, n), False, False)] +
+              [(o, l, r, False, i == len(payload) - 1) for i, (o, l, r) in enumerate(payload)])
+        else:
+            P([(R(K, 0, n), R("ONB", 0, 128), R(con, 0, n), True, False)] + [(o, l, r, False, False) for o, l, r in payload])
+            P([(R(K, k, n, 16), R(a, k, 2048, 16), R("BLK", 0, n // 16), False, k == m - 1) for k in range(m)])
+
+    I16, IB, INB = R("IW", 4, 132), R("IB", 4, 132), R("INB", 4, 132)
+    ISH = R("IW", 5, 133)
+    for t in range(3):
+        z = "z%d" % t
+        P([(R("b0", 8 * h, 8 * h + 8), R(z, 128 * h, 128 * h + 128), R("W8", 0, 8), True, True) for h in (0, 1)])
+        V(tc, R("ui", 0, 16), R("b0", 0, 16))
+        V(ts, R("ui", 0, 16), R("ui", 0, 16), 4095, None, A.bitwise_and)
+        V(tt, R("uu", 0, 16), R("ui", 0, 16), R("ui", 0, 16), A.mult)
+        V(ts, R("UQ", 0, 16), R("ui", 0, 16), 2047, None, A.bitwise_and)
+        V(ts, R("UQ", 16, 32), R("uu", 0, 16), 4, 2047, A.arith_shift_right, A.bitwise_and)
+        V(ts, R("UQ", 32, 48), R("uu", 0, 16), 5, 1023, A.arith_shift_right, A.bitwise_and)
+        V(tc, R("UH", 0, 48), R("UQ", 0, 48))
+        P([(R("b0", 128, 256, 1, 48), R("UH", 0, 48), I16, True, True)])
+        S(R("RLu", 0, 128, 1, 48), R("b0", 128, 256, 1, 48), F.Copy)
+        P([(R("b0", 256 + 128 * h, 384 + 128 * h), R("PM_%d" % h, 0, 128, 1, 48), R("RLu", 0, 128, 1, 48), True, True) for h in (0, 1)])
+        if t == 0:
+            V(tc, R("em", 0, 256), R("b0", 256, 512))
+        else:
+            V(ts, R("em", 0, 256), R("b0", 256, 512), c1("Ac"), None, A.add)
+        V(ts, R("em", 0, 256), R("em", 0, 256), 1023, None, A.bitwise_and)
+        V(tc, R("emu", 0, 256), R("em", 0, 256))
+        nz = opt["zv"][t]
+        VM(tc, [(R("zx", m, 4096, 16), R(z, 0, 256)) for m in range(nz)])
+        for m in range(nz, 16):
+            S(R("zx", m, 4096, 16), R(z, 0, 256), F.Copy)
+        V(tc, R("emh", 0, 256), R("emu", 0, 256))
+        for h in (0, 1):
+            H, K = "_%d" % h, "b%d" % (2 + h)
+            ch = opt["gchunk"]
+            w = 2048 // ch
+            for c in range(ch):
+                V(tt, R("DG" + H, w * c, w * c + w), ind(R("G", 0, 1024), R("emu", 128 * h + w // 16 * c, 128 * h + w // 16 * (c + 1))),
+                  R("zx", 2048 * h + w * c, 2048 * h + w * c + w), A.subtract)
+                size(opt["rg"][h], R("AG" + H, w * c, w * c + w), R("DG" + H, w * c, w * c + w))
+            keys(opt["rg"][h], K, 128, 16, "DG" + H, "AG" + H, "CD", "CDi", [(R(K, 0, 128), R("emh", 128 * h, 128 * h + 128), I16)])
+        if t == 0:
+            load_names()
+        for h in (0, 1):
+            H, K = "_%d" % h, "b%d" % (2 + h)
+            V("tensor_tensor_scan", R("km" + H, 0, 128), R("MMIN", 0, 128), R(K, 0, 128), 0.0, A.max, A.min)
+            V(tc, R("ei" + H, 0, 8), R("km" + H, 15, 128, 16))
+            V(ts, R("ej" + H, 0, 8), R("ei" + H, 0, 8), 1023, None, A.bitwise_and)
+            V(tt, R("ME" + H, 0, 128), ind(R("ej" + H, 0, 8), R("OFFR", 0, 8)), R("MK", 0, 128), A.mult)
+            P([(R("b7", 8 * h, 8 * h + 8), R("ME" + H, 0, 128), R("Q16", 0, 8), True, True)])
+            V(tc, R("eu" + H, 0, 8), R("b7", 8 * h, 8 * h + 8))
+            V(tc, R("Ju" + H, 0, 128), ind(R("I", 0, 1024), R("eu" + H, 0, 8)))
+            V(tc, R("Jh", 128 * h, 128 * h + 128), R("Ju" + H, 0, 128))
+            V(tc, R("e_rq", 8 * h, 8 * h + 8), R("eu" + H, 0, 8))
+            P([(R("b7", 256 + 128 * h, 384 + 128 * h), R("ME" + H, 0, 128), I16, True, True)])
+        if t == 0:
+            late_constants()
+            load_links()
+        for h in (0, 1):
+            H, K = "_%d" % h, "b%d" % (2 + h)
+            lk = ind(R("L", 0, 2048), R("Ju" + H, 0, 128))
+            xg = ind(R("xb", 0, 2048), R("Ju" + H, 0, 128))
+            if opt["lv"][h]:
+                V(tc, R("Lg" + H, 0, 2048), lk)
+            else:
+                S(R("Lg" + H, 0, 2048), lk, F.Copy)
+            if opt["xv"][h]:
+                V(tc, R("x" + H, 0, 2048), xg)
+            else:
+                S(R("x" + H, 0, 2048), xg, F.Copy)
+            P([(R("b6", 128 * h, 128 * h + 128), R("SEL", 128 * k, 128 * k + 128), R("Lg" + H, k, 2048, 16), k == 0, k == 15) for k in range(16)])
+            V(tc, R("nu" + H, 0, 128), R("b6", 128 * h, 128 * h + 128))
+            yc = opt["ychunk"]
+            w = 2048 // yc
+            for c in range(yc):
+                V(tt, R("Dy" + H, w * c, w * c + w), ind(R("xb", 0, 2048), R("nu" + H, w // 16 * c, w // 16 * (c + 1))), R("x" + H, w * c + 1, w * c + w + 1), A.subtract)
+                size(opt["ry"][h], R("Ay" + H, w * c, w * c + w), R("Dy" + H, w * c, w * c + w))
+            V("tensor_tensor_scan", R("mx" + H, 0, 2048), R("MR", 0, 2048), R("x" + H, 0, 2048), 0.0, A.mult, A.max)
+            for c in range(4):
+                B = "b%d" % (4 + c % 2)
+                P([(R(B, 0, 512), IB, R("x" + H, 512 * c, 512 * c + 512), True, False),
+                   (R(B, 0, 512), INB, R("zx", 2048 * h + 512 * c, 2048 * h + 512 * c + 512), False, True)])
+                S(R("Af" + H, 512 * c, 512 * c + 512), R(B, 0, 512), F.Abs)
+            P([(R("b1", 128 * h, 128 * h + 128), R("ZB", 15 - k, 143 - k), R("Af" + H, k, 2048, 16), k == 0, k == 15) for k in range(16)])
+            V(ts, R("far", 128 * h, 128 * h + 128), R("b1", 128 * h, 128 * h + 128), R("tf", 1, 2), None, A.is_gt)
+        P([(R("b6", 256 + 128 * h, 384 + 128 * h), IB, R(z, 128 * h, 128 * h + 128), True, False) if a == 0 else
+           (R("b6", 256 + 128 * h, 384 + 128 * h), IB, R("mx_%d" % h, 15, 2048, 16), False, True) for h in (0, 1) for a in (0, 1)])
+        S(R("zt", 0, 256), R("b6", 256, 512), F.Copy, 127.75, 0.5)
+        V(ts, R("zs%d" % t, 0, 256), R("zt", 0, 256), -128.0, None, A.add)
+        add("g", "remote", [(t,)], [R("zs%d" % t, 0, 256)], [R("z%d" % (t + 1), 0, 256)], 300, 4000)
+        S(R("Y", 0, 256), R("b7", 256, 512), F.Copy)
+        P([(R("b7", 256, 512), R("BH", 0, 128), R("Y", 0, 256), True, True)])
+        S(R("Er", 0, 256), R("b7", 256, 512), F.Copy)
+        dedupe("Er", None, lambda q: R("e_rq", q, q + 1), "EQE", "DUPE", "fl")
+        V(tt, R("of1", 0, 16), R("fl", 0, 16), R("DUE", 0, 16), A.mult)
+        V(tt, R("of2", 0, 16), R("of1", 0, 16), R("e_rq", 0, 16), A.max)
+        V(tc, R("oEu", 0, 16), R("of2", 0, 16))
+        P([(R("b0", 256 + 128 * h, 384 + 128 * h), R("PQ_%d" % h, 0, 128, 1, 48), R("RLu", 0, 128, 1, 48), True, True) for h in (0, 1)])
+        V(tc, R("vi", 0, 256), R("b0", 256, 512))
+        V(ts, R("vi", 0, 256), R("vi", 0, 256), 2047, None, A.bitwise_and)
+        S(R("Jf", 0, 256), R("Jh", 0, 256), F.Copy)
+        VJ = R("b3", 256, 512)
+        P([(R("b2", 256, 512), I16, R("Jh", 0, 256), True, True)])
+        V(tt, VJ, R("vi", 0, 256), R("b2", 256, 512), A.subtract)
+        for h in (0, 1):
+            H, K = "_%d" % h, "b%d" % (2 + h)
+            J = R("Jh", 128 * h, 128 * h + 128)
+            keys(opt["ry"][h], K, 256, 15, "Dy" + H, "Ay" + H, "CS", "CSi", [(R(K, 0, 128), J, I16), (R(K, 128, 256), J, ISH)])
+            V(tt, R("le" + H, 0, 128), R(K, 0, 128), R("THR", 0, 128), A.is_lt)
+            V("tensor_tensor_scan", R("sm" + H, 0, 256), R("MMAX", 0, 256), R(K, 0, 256), 0.0, A.min, A.max)
+            V("tensor_tensor_scan", R("cs" + H, 0, 128), R("MR", 0, 128), R("le" + H, 0, 128), 0.0, A.mult, A.add)
+            V(tc, R("si" + H, 0, 16), R("sm" + H, 15, 256, 16))
+            V(ts, R("QT" + H, 0, 8), R("cs" + H, 15, 128, 16), 11.5, None, A.is_gt)
+            V(ts, R("sj" + H, 0, 16), R("si" + H, 0, 16), 2047, None, A.bitwise_and)
+            V(ts, R("sj" + H, 16, 24), R("si" + H, 0, 8), 11, 15, A.arith_shift_right, A.bitwise_and)
+            V(tc, R("QT" + H, 8, 32), R("sj" + H, 0, 24))
+            P([(R("b1", 256 + 128 * h, 384 + 128 * h, 1, 32), R("QT" + H, 0, 32), I16, True, True)])
+            S(R("RL", 128 * h, 128 * h + 128, 1, 32), R("b1", 256 + 128 * h, 384 + 128 * h, 1, 32), F.Copy)
+        if t < 2:
+            P([(R("b7", 16, 24), R("ONH", 0, 128), R("QT_0", 0, 8), True, False), (R("b7", 16, 24), R("ONH", 0, 128), R("QT_1", 0, 8), False, True)])
+            V("tensor_reduce", c1("Ac"), R("b7", 16, 24), "X", A.add)
+        RL = R("RL", 0, 256, 1, 32)
+        P([(R("b4", 256, 512), R("RPJ", 0, 128, 1, 32), RL, True, True)])
+        P([(R("b4", 0, 256), R("RPR", 0, 128, 1, 32), RL, True, True)])
+        P([(R("b5", 0, 256), R("RPN", 0, 128, 1, 32), RL, True, True), (R("b5", 256, 512), R("RPK", 0, 128, 1, 32), RL, True, True)])
+        V(tt, R("mj", 0, 256), R("b4", 256, 512), R("MK", 0, 256), A.mult)
+        V(tt, R("ch", 0, 256), R("b4", 0, 256), R("far", 0, 256), A.max)
+        S(R("RJh", 0, 256), R("b4", 256, 512), F.Copy)
+        V("tensor_tensor_scan", R("scj", 0, 256), R("MR", 0, 256), R("mj", 0, 256), 0.0, A.mult, A.add)
+        JJ = R("scj", 15, 256, 16)
+        if t < 2:
+            V(ts, R("nr", 0, 16), JJ, 4095.5, None, A.is_lt)
+            V(tt, R("og1", 0, 16), R("nr", 0, 16), R("DUE", 0, 16), A.mult)
+            V(tt, R("og2", 0, 16), R("og1", 0, 16), R("of2", 0, 16), A.max)
+            V(tc, R("oGu", 0, 16), R("og2", 0, 16))
+            V(tc, ind(R("G", 0, 1280), R("oGu", 0, 16)), R(z, 0, 256))
+        V(tt, R("tmp", 0, 256), R("ch", 0, 256), VJ, A.mult)
+        V(tt, ind(R("I", 0, 1280), R("oEu", 0, 16)), R("tmp", 0, 256), R("Jf", 0, 256), A.add)
+        if t == 2:
+            dma("y", "yi", R("I", 0, 1024), 4096, "d8")
+        dedupe("RJh", None, lambda q: R("scj", 16 * q + 15, 16 * q + 16), "EQJ", "DUPJ", "flJ")
+        V(tt, R("oj1", 0, 16), R("flJ", 0, 16), R("DUJ", 0, 16), A.mult)
+        V(tt, R("oj2", 0, 16), R("oj1", 0, 16), JJ, A.max)
+        V(tt, R("oj3", 0, 16), R("oj2", 0, 16), R("DUJ", 0, 16), A.min)
+        V(tc, R("oJu", 0, 16), R("oj3", 0, 16))
+        S(R("Lold", 0, 256), ind(R("L", 0, 2304), R("oJu", 0, 16)), F.Copy)
+        V(ts, R("mk", 0, 256), R("b5", 256, 512), c1("k15"), None, A.is_equal)
+        V(tt, R("b5", 0, 256), R("b5", 0, 256), R("Lold", 0, 256), A.subtract)
+        V(tt, R("t2", 0, 256), R("b5", 0, 256), R("mk", 0, 256), A.mult)
+        V(tt, ind(R("L", 0, 2304), R("oJu", 0, 16)), R("t2", 0, 256), R("Lold", 0, 256), A.add)
+    dma("s", "yz", R("z3", 0, 256), 512, "d9")
+    dma("y", "yl", R("L", 0, 2048), 8192, "d10")
+    return ops
+
+
+def bank(r):
+    return r[0] if r[0][0] == "b" and len(r[0]) == 2 else None
+
+
+def edges(ops):
+    touched, pre = {}, []
+    for o in ops:
+        e = {}
+        for w, rs in ((True, o["writes"]), (False, o["reads"])):
+            for r in rs:
+                key = PLACE[r[0]][0] if False else r[0]
+                for (j, s, sw) in touched.get(key, []):
+                    same = ops[j]["q"] == o["q"]
+                    if bank(r):
+                        if not same:
+                            e[j] = True
+                        elif o["q"] == "t":
+                            e.setdefault(j, False)
+                        elif (w or sw) and clash(r, s):
+                            e[j] = e.get(j, False) or bool(sw)
+                    elif (w or sw) and clash(r, s):
+                        need = True if not same else (sw or ops[j]["kind"] == "dma")
+                        e[j] = e.get(j, False) or bool(need)
+        pre.append(e)
+        for w, rs in ((True, o["writes"]), (False, o["reads"])):
+            for r in rs:
+                touched.setdefault(r[0], []).append((o["i"], r, w))
+    return pre
+
+
+def label(o):
+    r = (o["writes"] or o["reads"])[0]
+    return o["q"] + r[0] + ("@%d" % r[1] if r[0][0] == "b" else "")
+
+
+def schedule(ops, pre, bias):
+    n = len(ops)
+    succ = [[] for _ in range(n)]
+    for i in range(n):
+        for j in pre[i]:
+            succ[j].append(i)
+    rankv = [0.0] * n
+    for i in range(n - 1, -1, -1):
+        o = ops[i]
+        b = 0.0
+        for k in succ[i]:
+            b = max(b, rankv[k] + (WAKE if pre[k][i] else 0.0))
+        rankv[i] = b + o["cost"] + o["lat"]
+    rankv = [rankv[i] + bias.get(label(ops[i]), 0.0) for i in range(n)]
+    left = [len(pre[i]) for i in range(n)]
+    ready = [0.0] * n
+    free = {}
+    avail = [i for i in range(n) if left[i] == 0]
+    order, start = [], [0.0] * n
+    while avail:
+        best = None
+        for i in avail:
+            s = max(ready[i], free.get(ops[i]["q"], 0.0))
+            key = (s, -rankv[i])
+            if best is None or key < best[0]:
+                best = (key, i)
+        s0, q = best[0][0], ops[best[1]]["q"]
+        i = best[1]
+        for k in avail:
+            if ops[k]["q"] == q and max(ready[k], free.get(q, 0.0)) <= s0 + 40 and rankv[k] > rankv[i]:
+                i = k
+        s = max(ready[i], free.get(q, 0.0))
+        avail.remove(i)
+        start[i] = s
+        free[q] = s + ops[i]["cost"]
+        order.append(i)
+        fin = s + ops[i]["cost"] + ops[i]["lat"]
+        for k in succ[i]:
+            ready[k] = max(ready[k], fin + (WAKE if pre[k][i] else 0.0) if pre[k][i] else s)
+            left[k] -= 1
+            if left[k] == 0:
+                avail.append(k)
+    return order, start
+
+
+OPT = {"gchunk": 1, "ychunk": 1, "lv": (0, 1), "xv": (0, 0), "zv": (0, 0, 0), "rg": (0, 0), "ry": (0, 0), "bias": {}}
+PLAN = {}
+
+
+def rank_program(g, core, T, topo):
+    rank = T.rank_of(core)
+    if rank is None:
+        return
+    if "ops" not in PLAN:
+        PLAN["ops"] = build(rank, OPT)
+        PLAN["pre"] = edges(PLAN["ops"])
+        PLAN["order"], PLAN["start"] = schedule(PLAN["ops"], PLAN["pre"], OPT["bias"])
+    ops, pre = PLAN["ops"], PLAN["pre"]
+    nxt = T.cores[(rank + 1) % len(T.cores)]
+    home = T.cores[(rank + 2) % len(T.cores)]
+    queue = {"v": g.vector, "s": g.scalar, "t": g.tensor, "g": g, "y": g.sync}
+    qsem = {"v": "qv", "s": "qs", "t": "qt", "g": "qg"}
+    count = {}
+    seen = {q: {} for q in queue}
+    done = {}
+
+    def ap(r):
+        if isinstance(r, IndOp):
+            return ap(r[0]).indirect(ap(r[1]))
+        name, off = PLACE[r[0]]
+        a, b, st, p = r[1] + off, r[2] + off, r[3], r[4]
+        t = T[name]
+        if st == 1:
+            return t[:, a:b] if p == 128 else t[0:p, a:b]
+        return t[:, a:b:st]
+
+    def arg(x):
+        return ap(x) if isinstance(x, tuple) else x
+
+    place = {i: n for n, i in enumerate(PLAN["order"])}
+    for i in PLAN["order"]:
+        o = ops[i]
+        q, eng = o["q"], queue[o["q"]]
+        known = seen[q]
+        for j in sorted(pre[i], key=lambda j: -place[j]):
+            if not pre[i][j]:
+                continue
+            sem, val, kn = done[j]
+            if known.get(sem, 0) < val:
+                eng.wait_ge(T.sem[sem], val)
+                for k in kn:
+                    known[k] = max(known.get(k, 0), kn[k])
+                known[sem] = max(known.get(sem, 0), val)
+        if o["kind"] == "dma":
+            out, in_ = o["calls"][0]
+            out = ap(out) if isinstance(out, tuple) else T[out][:]
+            in_ = ap(in_) if isinstance(in_, tuple) else T[in_][:]
+            eng.dma_start(out, in_).then_inc(T.sem[o["sem"]], 16)
+            done[i] = (o["sem"], 16, dict(known))
+            count[o["sem"]] = 16
+            continue
+        if o["kind"] == "remote":
+            t = o["calls"][0][0]
+            dst = nxt if t < 2 else home
+            rid, pid, _e = topo.addr(dst)
+            g.remote_dma(T["z%d" % (t + 1)][:], T["zs%d" % t][:], T.sem["arr%d" % (t + 1)], T.sem["loc"], pid, rid, topo.mask(core, dst))
+            m = len(topo.engines(core, dst))
+            src = T.cores[(rank - 1) % len(T.cores)] if t < 2 else T.cores[(rank - 2) % len(T.cores)]
+            count["loc"] = count.get("loc", 0) + m
+            done[i] = ("arr%d" % (t + 1), len(topo.engines(src, core)), {})
+            continue
+        sem = qsem[q]
+        for c in o["calls"]:
+            if o["kind"] == "matmul":
+                ins = g.tensor.matmul(ap(c[0]), ap(c[1]), ap(c[2]), c[3], c[4])
+            elif o["kind"] == "activation":
+                kw = {}
+                if c[3] is not None:
+                    kw["bias"] = arg(c[3])
+                if c[4] is not None:
+                    kw["scale"] = arg(c[4])
+                ins = g.scalar.activation(ap(c[0]), ap(c[1]), c[2], **kw)
+            elif o["kind"] == "iota":
+                ins = g.iota(ap(c[0]), c[1], c[2], c[3])
+            else:
+                x = [arg(y) for y in c]
+                k = o["kind"]
+                if k == "tensor_copy":
+                    ins = g.vector.tensor_copy(*x)
+                elif k == "tensor_scalar":
+                    ins = g.vector.tensor_scalar(*x)
+                elif k == "tensor_tensor":
+                    ins = g.vector.tensor_tensor(*x)
+                elif k == "tensor_tensor_scan":
+                    ins = g.vector.tensor_tensor_scan(*x)
+                elif k == "tensor_reduce":
+                    ins = g.vector.tensor_reduce(x[0], x[1], AxisListType.X, x[3])
+                else:
+                    ins = g.vector.memset(*x)
+            ins.then_inc(T.sem[sem], 1)
+            count[sem] = count.get(sem, 0) + 1
+        kn = dict(known)
+        kn[sem] = count[sem]
+        done[i] = (sem, count[sem], kn)
+    for sem in sorted(count):
+        g.wait_ge(T.sem[sem], count[sem])

@@ -36,7 +36,7 @@ for _n, _c, _d in (
         ("C0", 256, "bfloat16"), ("BL2", 16, "bfloat16"), ("BLN", 16, "bfloat16"), ("CDi", 128, "bfloat16"), ("CSi", 256, "bfloat16"),
         ("ui", 16, "int32"), ("uu", 16, "int32"), ("UQ", 48, "int32"), ("UH", 48, "float16"), ("RLu", 128, "float16"), ("em", 256, "int32"), ("emu", 256, "uint16"), ("emh", 256, "float16"),
         ("sh4", 256, "int32"), ("vi", 256, "int32"), ("vJ", 256, "float32"), ("Jf", 256, "float32"), ("Jh", 256, "float16"),
-        ("zx", 4096, "bfloat16"), ("e_rq", 16, "float32"), ("Y", 256, "float16"), ("Er", 256, "float16"),
+        ("zx0", 4096, "bfloat16"), ("zx1", 4096, "bfloat16"), ("e_rq", 16, "float32"), ("Y", 256, "float16"), ("Er", 256, "float16"),
         ("far", 256, "float32"), ("ch", 256, "float32"), ("tmp", 256, "float32"), ("RL", 256, "float16"), ("RJh", 256, "float16"),
         ("mj", 256, "float32"), ("scj", 256, "float32"), ("EQE", 2176, "bfloat16"), ("DUPE", 2176, "bfloat16"),
         ("EQJ", 2176, "bfloat16"), ("DUPJ", 2176, "bfloat16"), ("fl", 16, "float32"), ("of1", 16, "float32"), ("of2", 16, "float32"),
@@ -330,9 +330,10 @@ def build(rank, opt):
         V(ts, R("em", 0, 256), R("em", 0, 256), 1023, None, A.bitwise_and)
         V(tc, R("emu", 0, 256), R("em", 0, 256))
         nz = opt["zv"][t]
-        VM(tc, [(R("zx", m, 4096, 16), R(z, 0, 256)) for m in range(nz)])
+        zx = "zx%d" % (t % 2)
+        VM(tc, [(R(zx, m, 4096, 16), R(z, 0, 256)) for m in range(nz)])
         for m in range(nz, 16):
-            S(R("zx", m, 4096, 16), R(z, 0, 256), F.Copy)
+            S(R(zx, m, 4096, 16), R(z, 0, 256), F.Copy)
         V(tc, R("emh", 0, 256), R("emu", 0, 256))
         for h in (0, 1):
             H, K = "_%d" % h, "b%d" % (2 + h)
@@ -340,7 +341,7 @@ def build(rank, opt):
             w = 2048 // ch
             for c in range(ch):
                 V(tt, R("DG" + H, w * c, w * c + w), ind(R("G", 0, 1024), R("emu", 128 * h + w // 16 * c, 128 * h + w // 16 * (c + 1))),
-                  R("zx", 2048 * h + w * c, 2048 * h + w * c + w), A.subtract)
+                  R(zx, 2048 * h + w * c, 2048 * h + w * c + w), A.subtract)
                 size(opt["rg"][h], R("AG" + H, w * c, w * c + w), R("DG" + H, w * c, w * c + w))
             keys(opt["rg"][h], K, 128, 16, "DG" + H, "AG" + H, "CD", "CDi", [(R(K, 0, 128), R("emh", 128 * h, 128 * h + 128), I16)])
         if t == 0:
@@ -380,13 +381,6 @@ def build(rank, opt):
                 V(tt, R("Dy" + H, w * c, w * c + w), ind(R("xb", 0, 2048), R("nu" + H, w // 16 * c, w // 16 * (c + 1))), R("x" + H, w * c + 1, w * c + w + 1), A.subtract)
                 size(opt["ry"][h], R("Ay" + H, w * c, w * c + w), R("Dy" + H, w * c, w * c + w))
             V("tensor_tensor_scan", R("mx" + H, 0, 2048), R("MR", 0, 2048), R("x" + H, 0, 2048), 0.0, A.mult, A.max)
-            for c in range(4):
-                B = "b%d" % (4 + c % 2)
-                P([(R(B, 0, 512), IB, R("x" + H, 512 * c, 512 * c + 512), True, False),
-                   (R(B, 0, 512), INB, R("zx", 2048 * h + 512 * c, 2048 * h + 512 * c + 512), False, True)])
-                S(R("Af" + H, 512 * c, 512 * c + 512), R(B, 0, 512), F.Abs)
-            P([(R("b1", 128 * h, 128 * h + 128), R("ZB", 15 - k, 143 - k), R("Af" + H, k, 2048, 16), k == 0, k == 15) for k in range(16)])
-            V(ts, R("far", 128 * h, 128 * h + 128), R("b1", 128 * h, 128 * h + 128), R("tf", 1, 2), None, A.is_gt)
         P([(R("b6", 256 + 128 * h, 384 + 128 * h), IB, R(z, 128 * h, 128 * h + 128), True, False) if a == 0 else
            (R("b6", 256 + 128 * h, 384 + 128 * h), IB, R("mx_%d" % h, 15, 2048, 16), False, True) for h in (0, 1) for a in (0, 1)])
         S(R("zt", 0, 256), R("b6", 256, 512), F.Copy, 127.75, 0.5)
@@ -418,18 +412,16 @@ def build(rank, opt):
             V(ts, R("sj" + H, 0, 16), R("si" + H, 0, 16), 2047, None, A.bitwise_and)
             V(ts, R("sj" + H, 16, 24), R("si" + H, 0, 8), 11, 15, A.arith_shift_right, A.bitwise_and)
             V(tc, R("QT" + H, 8, 32), R("sj" + H, 0, 24))
-            P([(R("b1", 256 + 128 * h, 384 + 128 * h, 1, 32), R("QT" + H, 0, 32), I16, True, True)])
-            S(R("RL", 128 * h, 128 * h + 128, 1, 32), R("b1", 256 + 128 * h, 384 + 128 * h, 1, 32), F.Copy)
+            P([(R("b7", 128, 256, 1, 32), R("QT" + H, 0, 32), I16, True, True)])
+            S(R("RL", 128 * h, 128 * h + 128, 1, 32), R("b7", 128, 256, 1, 32), F.Copy)
         if t < 2:
             P([(R("b7", 16, 24), R("ONH", 0, 128), R("QT_0", 0, 8), True, False), (R("b7", 16, 24), R("ONH", 0, 128), R("QT_1", 0, 8), False, True)])
             V("tensor_reduce", c1("Ac"), R("b7", 16, 24), "X", A.add)
         RL = R("RL", 0, 256, 1, 32)
-        P([(R("b4", 256, 512), R("RPJ", 0, 128, 1, 32), RL, True, True)])
-        P([(R("b4", 0, 256), R("RPR", 0, 128, 1, 32), RL, True, True)])
-        P([(R("b5", 0, 256), R("RPN", 0, 128, 1, 32), RL, True, True), (R("b5", 256, 512), R("RPK", 0, 128, 1, 32), RL, True, True)])
-        V(tt, R("mj", 0, 256), R("b4", 256, 512), R("MK", 0, 256), A.mult)
-        V(tt, R("ch", 0, 256), R("b4", 0, 256), R("far", 0, 256), A.max)
-        S(R("RJh", 0, 256), R("b4", 256, 512), F.Copy)
+        P([(R("b6", 256, 512), R("RPJ", 0, 128, 1, 32), RL, True, True)])
+        V(tt, R("mj", 0, 256), R("b6", 256, 512), R("MK", 0, 256), A.mult)
+        S(R("RJh", 0, 256), R("b6", 256, 512), F.Copy)
+        P([(R("b6", 0, 256), R("RPN", 0, 128, 1, 32), RL, True, True), (R("b6", 256, 512), R("RPK", 0, 128, 1, 32), RL, True, True)])
         V("tensor_tensor_scan", R("scj", 0, 256), R("MR", 0, 256), R("mj", 0, 256), 0.0, A.mult, A.add)
         JJ = R("scj", 15, 256, 16)
         if t < 2:
@@ -438,6 +430,17 @@ def build(rank, opt):
             V(tt, R("og2", 0, 16), R("og1", 0, 16), R("of2", 0, 16), A.max)
             V(tc, R("oGu", 0, 16), R("og2", 0, 16))
             V(tc, ind(R("G", 0, 1280), R("oGu", 0, 16)), R(z, 0, 256))
+        for h in (0, 1):
+            H = "_%d" % h
+            for c in range(4):
+                B = "b%d" % (4 + c % 2)
+                P([(R(B, 0, 512), IB, R("x" + H, 512 * c, 512 * c + 512), True, False),
+                   (R(B, 0, 512), INB, R(zx, 2048 * h + 512 * c, 2048 * h + 512 * c + 512), False, True)])
+                S(R("Af" + H, 512 * c, 512 * c + 512), R(B, 0, 512), F.Abs)
+            P([(R("b1", 128 * h, 128 * h + 128), R("ZB", 15 - k, 143 - k), R("Af" + H, k, 2048, 16), k == 0, k == 15) for k in range(16)])
+            V(ts, R("far", 128 * h, 128 * h + 128), R("b1", 128 * h, 128 * h + 128), R("tf", 1, 2), None, A.is_gt)
+        P([(R("b1", 256, 512), R("RPR", 0, 128, 1, 32), RL, True, True)])
+        V(tt, R("ch", 0, 256), R("b1", 256, 512), R("far", 0, 256), A.max)
         V(tt, R("tmp", 0, 256), R("ch", 0, 256), VJ, A.mult)
         V(tt, ind(R("I", 0, 1280), R("oEu", 0, 16)), R("tmp", 0, 256), R("Jf", 0, 256), A.add)
         if t == 2:
@@ -448,9 +451,9 @@ def build(rank, opt):
         V(tt, R("oj3", 0, 16), R("oj2", 0, 16), R("DUJ", 0, 16), A.min)
         V(tc, R("oJu", 0, 16), R("oj3", 0, 16))
         S(R("Lold", 0, 256), ind(R("L", 0, 2304), R("oJu", 0, 16)), F.Copy)
-        V(ts, R("mk", 0, 256), R("b5", 256, 512), c1("k15"), None, A.is_equal)
-        V(tt, R("b5", 0, 256), R("b5", 0, 256), R("Lold", 0, 256), A.subtract)
-        V(tt, R("t2", 0, 256), R("b5", 0, 256), R("mk", 0, 256), A.mult)
+        V(ts, R("mk", 0, 256), R("b6", 256, 512), c1("k15"), None, A.is_equal)
+        V(tt, R("b6", 0, 256), R("b6", 0, 256), R("Lold", 0, 256), A.subtract)
+        V(tt, R("t2", 0, 256), R("b6", 0, 256), R("mk", 0, 256), A.mult)
         V(tt, ind(R("L", 0, 2304), R("oJu", 0, 16)), R("t2", 0, 256), R("Lold", 0, 256), A.add)
     dma("s", "yz", R("z3", 0, 256), 512, "d9")
     dma("y", "yl", R("L", 0, 2048), 8192, "d10")
@@ -537,7 +540,11 @@ def schedule(ops, pre, bias):
     return order, start
 
 
-OPT = {"gchunk": 1, "ychunk": 1, "lv": (0, 1), "xv": (0, 0), "zv": (0, 0, 0), "rg": (0, 0), "ry": (0, 0), "bias": {}}
+URGE = """
+vmk:-5 vDUPE:-1 vb6@0:-10 tb1@0:-16 vCS:31 sAy_1:-8 vONH:-16 vmx_0:-6 vI:-11 ve_rq:8 vp16i:9 szx1:-5 vx_1:13 vQ16:15 vUQ:-19 sAf_1:-8 vpk1:-21 vDUE:7 vDUPJ:-4 vmx_1:-5 vMMIN:-9 vBLK:8 tb6@256:25 szx0:-16 tb6@0:29 sAy_0:-4 vle_0:1 vch:6 tb5@0:4 vkm_0:17 vDy_1:-2 vk15:12 voEu:-19 sDM:2 vJh:4 vsi_0:5 vRPR:13 vp16:8 shki:-7 vRPN:13 vej_0:-5 vvi:4 vEQE:1 vL:6 gz1:2 yG:-15 vIW:-4 vsm_1:4 vpk3:4 yixi:3 vle_1:2 vOWN:-8 vsi_1:9 vsj_1:-1 yL:23 tb4@0:-5 gduI:7 vzs0:-3 sAG_1:1 vDG_0:-6 yxb:4 vzx0:-14 vZQ:-10 vemh:-1 vtf:-11 ylki:-12 vzs2:-11 gdI:2 tb7@16:-9 vej_1:2 vzx1:-1 vZB:1 vKM:2 sRL:3 vG:4 vMMAX:5 tb6@128:16 vDG_1:-5 vME_1:-4 vscj:-5 vUH:-10 gz3:-9 vBLN:-6 yz0:-4 vsj_0:1 vpk2:4 vPICK:2 sL:4 vnu_1:7 sJf:1 vONB:3 vEQJ:5 veu_0:9 voJu:-3 vx_0:-4 vW8:9 vINB:-1 voj3:2 vRPK:-3 vOFFR:8 gr15I:-1 vJu_0:-4 vCD:-6 voj2:-5 vt2:1 vDy_0:6 tb4@256:6 vIB:-6 tb1@128:6 vQT_1:-1 sx_0:3 tb7@128:3 grI:-7 sPQ_1:3 vTHR:-4 vDM:-1 sz3:-8 veu_1:-4 vfl:1 vdgA:-3 vuu:-1 vAc:5 vcs_1:-1 vME_0:-3 tb2@256:-10 szt:1 voj1:1 vmj:-1 vnr:-2 gdgI:3 sEr:6 vwf:-1 sLg_0:-3 vMK:3 gz2:3 gcI:3 sRLu:-5 sRJh:3 vzs1:-1 tb0@0:5 vog2:-3 sthi:-5 vkm_1:1 ggI:8 vof1:5 sAG_0:-1 tb7@8:-3 sLold:1
+"""
+OPT = {"gchunk": 1, "ychunk": 4, "lv": (0, 0), "xv": (0, 1), "zv": (0, 0, 0), "rg": (0, 0), "ry": (0, 0),
+       "bias": {w.split(":")[0]: 500.0 * int(w.split(":")[1]) for w in URGE.split()}}
 PLAN = {}
 
 

import numpy as np
from concourse.mybir import AluOpType as A, AxisListType, ActivationFunctionType as F

BIG = 1.0e9
OFF24 = 16777216.0
CYC = 0.8333
GAT, SCA, WAKE, FIX = 1.56, 3.8, 70.0, 20.0
SCRATCH, SIZES = {}, {}
TWO = ("bfloat16", "float16", "uint16")


def _buf(name, cols, dtype, where="sbuf"):
    SCRATCH[name] = (where, [128, cols], dtype)


for _n, _c, _d in (
        ("xb", 2048, "bfloat16"), ("G", 1280, "bfloat16"), ("ixi", 1024, "int32"), ("I", 1280, "float32"),
        ("lki", 2048, "int32"), ("L", 2304, "float32"),
        ("wti", 1, "int32"), ("hki", 2, "int32"), ("thi", 2, "int32"),
        ("z0", 256, "bfloat16"), ("z1", 256, "bfloat16"), ("z2", 256, "bfloat16"), ("z3", 256, "bfloat16"),
        ("zs0", 256, "bfloat16"), ("zs1", 256, "bfloat16"), ("zs2", 256, "bfloat16"), ("zt", 256, "bfloat16"),
        ("pI", 1, "int32"), ("p16i", 1, "int32"), ("pgi", 1, "int32"), ("pf", 1, "float32"), ("p16", 1, "float32"),
        ("pg", 1, "float32"), ("pz", 1, "float32"), ("colA", 1, "float32"), ("colB", 1, "float32"), ("k15", 1, "float32"),
        ("wf", 1, "float32"), ("hf", 2, "float32"), ("tf", 2, "float32"),
        ("dI", 144, "int32"), ("cI", 144, "int32"), ("gI", 128, "int32"), ("g8I", 16, "int32"), ("rI", 256, "int32"),
        ("dgI", 128, "int32"), ("duI", 16, "int32"), ("r15I", 256, "int32"),
        ("IW", 136, "float16"), ("IB", 136, "bfloat16"), ("INB", 136, "bfloat16"), ("BB", 128, "bfloat16"), ("BH", 128, "float16"),
        ("BLK", 16, "bfloat16"), ("Q16", 8, "float16"), ("MK", 256, "float16"), ("ZB", 144, "bfloat16"),
        ("SEL", 2048, "float16"), ("KM", 16, "float32"), ("CD", 128, "bfloat16"), ("CS", 256, "bfloat16"),
        ("ONB", 128, "bfloat16"), ("ONH", 128, "float16"), ("MMIN", 128, "float32"), ("MMAX", 256, "float32"),
        ("MR", 2048, "bfloat16"), ("OFFR", 8, "uint16"), ("pk1", 1, "float32"), ("pk2", 1, "float32"), ("pk3", 1, "float32"),
        ("PICK", 2, "uint16"), ("DUE", 16, "float32"), ("DUJ", 16, "float32"), ("DM", 2176, "bfloat16"), ("OWN", 16, "bfloat16"),
        ("RPR", 128, "float16"), ("RPJ", 128, "float16"), ("RPt", 128, "float16"), ("RPN", 128, "float16"), ("RPK", 128, "float16"),
        ("dgA", 128, "float16"), ("THR", 128, "float32"), ("Wb", 128, "bfloat16"),
        ("W8", 8, "bfloat16"), ("ZQ", 200, "float16"), ("PM_0", 128, "float16"), ("PM_1", 128, "float16"), ("PQ_0", 128, "float16"), ("PQ_1", 128, "float16"),
        ("C0", 256, "bfloat16"), ("BL2", 16, "bfloat16"), ("BLN", 16, "bfloat16"), ("CDi", 128, "bfloat16"), ("CSi", 256, "bfloat16"),
        ("ui", 16, "int32"), ("uu", 16, "int32"), ("UQ", 48, "int32"), ("UH", 48, "float16"), ("RLu", 128, "float16"), ("em", 256, "int32"), ("emu", 256, "uint16"), ("emh", 256, "float16"),
        ("sh4", 256, "int32"), ("vi", 256, "int32"), ("vJ", 256, "float32"), ("Jf", 256, "float32"), ("Jh", 256, "float16"),
        ("zx0", 4096, "bfloat16"), ("zx1", 4096, "bfloat16"), ("e_rq", 16, "float32"), ("Y", 256, "float16"), ("Er", 256, "float16"),
        ("far", 256, "float32"), ("ch", 256, "float32"), ("tmp", 256, "float32"), ("RL", 256, "float16"), ("RJh", 256, "float16"),
        ("mj", 256, "float32"), ("scj", 256, "float32"), ("EQE", 2176, "bfloat16"), ("DUPE", 2176, "bfloat16"),
        ("EQJ", 2176, "bfloat16"), ("DUPJ", 2176, "bfloat16"), ("fl", 16, "float32"), ("of1", 16, "float32"), ("of2", 16, "float32"),
        ("nr", 16, "float32"), ("og1", 16, "float32"), ("og2", 16, "float32"), ("flJ", 16, "float32"), ("oj1", 16, "float32"),
        ("oj2", 16, "float32"), ("oj3", 16, "float32"), ("oEu", 16, "uint16"), ("oGu", 16, "uint16"), ("oJu", 16, "uint16"),
        ("Lold", 256, "float32"), ("mk", 256, "float32"), ("t1", 256, "float32"), ("t2", 256, "float32"), ("Ac", 1, "float32")):
    _buf(_n, _c, _d)
for _h in "01":
    for _n, _c, _d in (("DG", 2048, "bfloat16"), ("AG", 2048, "bfloat16"), ("x", 2064, "bfloat16"), ("Lg", 2048, "float16"), ("mx", 2048, "bfloat16"),
                       ("Dy", 2048, "bfloat16"), ("Ay", 2048, "bfloat16"), ("Af", 2048, "bfloat16"), ("km", 128, "float32"),
                       ("ei", 8, "int32"), ("ej", 8, "int32"), ("ME", 128, "float16"), ("eu", 8, "uint16"), ("Ju", 128, "uint16"), ("nu", 128, "uint16"),
                       ("le", 128, "bfloat16"), ("cs", 128, "bfloat16"), ("sm", 256, "float32"), ("si", 16, "int32"), ("sj", 24, "int32"), ("QT", 32, "float16")):
        _buf(_n + "_" + _h, _c, _d)
for _b in range(8):
    _buf("b%d" % _b, 512, "float32", "psum")
PLACE = {}
_pack = {}
for _n in sorted(SCRATCH):
    _w, _s, _d = SCRATCH[_n]
    if _w == "sbuf" and _n not in ("xb", "G", "I", "L", "ixi", "lki", "z0", "z1", "z2", "z3", "zs0", "zs1", "zs2") and _s[1] < 2000:
        _o = _pack.get(_d, 0)
        PLACE[_n] = ("k_" + _d, _o)
        _pack[_d] = _o + (_s[1] + 31) // 32 * 32
    else:
        PLACE[_n] = (_n, 0)
DTYPE = {_n: SCRATCH[_n][2] for _n in SCRATCH}
for _n in list(SCRATCH):
    if PLACE[_n][0] != _n:
        del SCRATCH[_n]
for _d in _pack:
    _buf("k_" + _d, _pack[_d], _d)
SEMAPHORES = ["qv", "qs", "qt", "qg", "loc", "arr1", "arr2", "arr3"] + ["d%d" % i for i in range(16)]


def R(buf, a=0, b=None, step=1, p=128):
    if b is None:
        b = a + 1
    return (buf, a, b, step, p)


def width(r):
    return (r[2] - r[1] + r[3] - 1) // r[3]


def clash(r, s):
    if r[0] != s[0] or r[1] >= s[2] or s[1] >= r[2]:
        return False
    return not (r[3] == s[3] and r[3] > 1 and (r[1] - s[1]) % r[3] != 0)


class IndOp(tuple):
    pass


def ind(win, off):
    return IndOp((win, off))


def build(rank, opt):
    ops, loaded = [], [0.0]

    def add(q, kind, calls, reads, writes, cost, lat=0.0, **kw):
        ops.append(dict(q=q, kind=kind, calls=calls, reads=reads, writes=writes, cost=cost, lat=lat, i=len(ops), **kw))

    def flat(x):
        if isinstance(x, IndOp):
            return [x[0], x[1]]
        return [x] if isinstance(x, tuple) else []

    def small(rs):
        return all(DTYPE[r[0]] in TWO for r in rs)

    def price(n, half=False, mult=1.0):
        return max(64.0, n * (0.5 if half else 1.0) * mult) * CYC + FIX

    def V(name, out, *args):
        full = [x for x in args if isinstance(x, tuple)]
        rd = [y for x in full for y in flat(x)]
        wr = flat(out)[:1]
        if isinstance(out, IndOp):
            rd = rd + [out[1]]
            n = width(out[1]) * 16
            c = 50 + n * SCA * CYC
        elif any(isinstance(x, IndOp) for x in full):
            c = 50 + width(out) * GAT * CYC
        elif name == "tensor_tensor":
            ps = any(x[0][0] == "b" and len(x[0]) == 2 for x in full)
            c = price(width(out), False, 1.0 if ps else 2.0)
        elif name == "tensor_reduce":
            c = price(width(args[0]))
        else:
            c = price(width(out), small([out] + [x for x in full if width(x) > 1]))
        add("v", name, [(out,) + args], rd, wr, c)

    def VM(name, items):
        if not items:
            return
        n0 = len(ops)
        for it in items:
            V(name, *it)
        got = ops[n0:]
        del ops[n0:]
        add("v", name, [o["calls"][0] for o in got], [r for o in got for r in o["reads"]], [r for o in got for r in o["writes"]], sum(o["cost"] for o in got))

    def S(out, in_, func, bias=None, scale=None):
        c = (65 + width(out) * GAT * CYC) if isinstance(in_, IndOp) else width(out) * CYC + 60
        rd = flat(in_) + [x for x in (bias, scale) if isinstance(x, tuple)]
        add("s", "activation", [(out, in_, func, bias, scale)], rd, [out], c)

    def P(items):
        c = 0.0
        for o, l, r, a, b in items:
            f32 = DTYPE[l[0]] == "float32"
            c += max(min(64, width(l)), width(r)) * (4 if f32 else 1) * CYC + 5
        rd, wr = [], []
        for o, l, r, a, b in items:
            for x in (l, r):
                if x not in rd:
                    rd.append(x)
            if o not in wr:
                wr.append(o)
        add("t", "matmul", items, rd, wr, c)

    def iota(out, pattern, base, cm):
        add("g", "iota", [(out, pattern, base, cm)], [], [out], 130 + 2 * width(out) * CYC)

    def dma(q, out, in_, nbytes, sem):
        rd = [in_] if isinstance(in_, tuple) else []
        wr = [out] if isinstance(out, tuple) else []
        loaded[0] += nbytes * 128 / 200.0 if wr else 0.0
        add(q, "dma", [(out, in_)], rd, wr, 60, 2000 + (loaded[0] if wr else nbytes * 128 / 200.0), sem=sem)

    dma("y", R("z0", 0, 256), "zc", 512, "d0")
    dma("s", R("wti", 0, 1), "wt", 4, "d1")
    dma("s", R("hki", 0, 2), "hk", 8, "d2")
    dma("y", R("G", 0, 1024), "gi", 2048, "d3")
    dma("y", R("ixi", 0, 1024), "ix", 4096, "d4")
    dma("y", R("xb", 0, 2048), "xc", 4096, "d5")
    dma("s", R("thi", 0, 2), "th", 8, "d6")
    dma("y", R("lki", 0, 2048), "lk", 8192, "d7")
    iota(R("pI", 0, 1), [[0, 1]], 0, 1)
    iota(R("gI", 0, 128), [[1, 8], [0, 16]], 0, 0)
    iota(R("dI", 0, 144), [[1, 144]], 0, -1)
    iota(R("g8I", 0, 16), [[0, 2], [1, 8]], 0, 0)
    iota(R("rI", 0, 256), [[0, 16], [1, 16]], 0, 0)
    iota(R("cI", 0, 144), [[1, 144]], 0, 0)
    iota(R("r15I", 0, 256), [[0, 16], [-1, 16]], 15, 0)
    iota(R("duI", 0, 16), [[16, 16]], 0, 0)
    iota(R("dgI", 0, 128), [[1, 8], [0, 16]], 0, -1)
    c1 = lambda b: R(b, 0, 1)
    ts, tt, tc = "tensor_scalar", "tensor_tensor", "tensor_copy"
    V(ts, c1("pgi"), c1("pI"), 4, None, A.arith_shift_right)
    V(tc, c1("pg"), c1("pgi"))
    V(tc, c1("wf"), c1("wti"))
    V(ts, R("W8", 0, 8), R("g8I", 0, 8), c1("pg"), c1("wf"), A.is_equal, A.mult)
    V(tc, R("hf", 0, 2), R("hki", 0, 2))
    V("memset", R("ZQ", 0, 200), 0.0)
    V(ts, R("ZQ", 48, 56), R("g8I", 0, 8), c1("pg"), None, A.is_equal)
    V(ts, R("ZQ", 152, 160), R("g8I", 0, 8), c1("pg"), 0.0625, A.is_equal, A.mult)
    V(ts, R("BH", 0, 128), R("gI", 0, 128), c1("pg"), None, A.is_equal)
    V(ts, c1("p16i"), c1("pI"), 15, None, A.bitwise_and)
    V(tc, c1("p16"), c1("p16i"))
    V(tc, c1("pf"), c1("pI"))
    V(ts, R("IW", 0, 136), R("dI", 0, 136), 4.0, None, A.is_equal)
    V(ts, R("BLK", 0, 16), R("g8I", 0, 16), c1("pg"), 32768.0, A.is_equal, A.mult)
    V(ts, R("Q16", 0, 8), R("g8I", 0, 8), c1("pg"), None, A.is_equal)
    V(ts, R("MK", 0, 256), R("rI", 0, 256), c1("p16"), None, A.is_equal)
    V(tc, R("OFFR", 0, 8), R("g8I", 0, 8))
    V(ts, c1("colA"), c1("pf"), 64.0, 32.0, A.is_ge, A.mult)
    V(ts, c1("colB"), c1("pf"), 64.0, -262144.0, A.is_lt, A.mult)
    V("memset", R("ONB", 0, 128), 1.0)
    V(ts, R("CD", 0, 128), R("rI", 0, 128), c1("colA"), c1("colB"), A.mult, A.add)
    V(ts, R("mj", 0, 256), R("rI", 0, 256), 0.0, 2 * BIG, A.is_equal, A.mult)
    V(ts, R("MMIN", 0, 128), R("mj", 0, 128), -BIG, None, A.add)
    V("memset", c1("pz"), 0.0)

    def factors(j, name, at):
        V(ts, R("dgA", 0, 128), R("IW", 4, 132), R("hf", j, j + 1), None, A.mult)
        for h in (0, 1):
            o = R("b4", 128 + 128 * h, 256 + 128 * h, 1, 48)
            P([(o, R("ZQ", 48 - 8 * h, 96 - 8 * h), R("dgA", 0, 128), True, False), (o, R("ZQ", at - 8 * h, at + 48 - 8 * h), R("BH", 0, 128), False, True)])
            S(R(name + str(h), 0, 128, 1, 48), o, F.Copy)
    factors(0, "PM_", 120)
    if any(opt["rg"]):
        V("memset", R("C0", 0, 256), -131072.0)
        V(ts, R("BL2", 0, 16), R("BLK", 0, 16), 2.0, None, A.mult)
        V(ts, R("BLN", 0, 16), R("BLK", 0, 16), -1.0, None, A.mult)
        V(ts, R("CDi", 0, 128), R("rI", 0, 128), c1("colA"), None, A.mult)

    def load_names():
        V(tc, R("I", 0, 1024), R("ixi", 0, 1024))

    def load_links():
        V("memset", R("L", 2048, 2304), 0.0)
        S(R("L", 0, 1024), R("lki", 0, 1024), F.Copy)
        S(R("L", 1024, 2048), R("lki", 1024, 2048), F.Copy)

    def late_constants():
        V(ts, R("IB", 0, 136), R("dI", 0, 136), 4.0, None, A.is_equal)
        V(ts, R("INB", 0, 136), R("dI", 0, 136), 4.0, -1.0, A.is_equal, A.mult)
        V(ts, R("KM", 0, 16), R("rI", 0, 16), c1("p16"), None, A.is_equal)
        for k in range(16):
            S(R("SEL", 128 * k, 128 * k + 128), R("IW", 4, 132), F.Copy, None, R("KM", k, k + 1))
        V("memset", R("MR", 0, 2048), 1.0)
        V("memset", R("MR", 0, 2048, 16), 0.0)
        V("memset", R("x_0", 2048, 2064), 0.0)
        V("memset", R("x_1", 2048, 2064), 0.0)
        V(ts, c1("pk3"), c1("pg"), 16.0, 15.0, A.mult, A.add)
        V(ts, R("ZB", 0, 144), R("cI", 0, 144), c1("pk3"), None, A.is_equal)
        V(ts, R("CS", 0, 256), R("r15I", 0, 256), c1("colA"), c1("colB"), A.mult, A.add)
        V(ts, R("MMAX", 0, 256), R("mj", 0, 256), -1.0, BIG, A.mult, A.add)
        V(tc, R("tf", 0, 2), R("thi", 0, 2))
        V("memset", R("ONH", 0, 128), 1.0)
        V(ts, R("dgA", 0, 128), R("IW", 4, 132), R("tf", 0, 1), None, A.mult)
        P([(R("b4", 0, 128), R("ONH", 0, 128), R("dgA", 0, 128), True, True)])
        V(ts, R("THR", 0, 128), R("b4", 0, 128), 32768.0, 32768.0 - OFF24, A.mult, A.add)
        V("memset", R("THR", 15, 128, 16), -2.0e7)
        factors(1, "PQ_", 136)
        if not any(opt["rg"]):
            V("memset", R("C0", 0, 256), -131072.0)
            V(ts, R("BL2", 0, 16), R("BLK", 0, 16), 2.0, None, A.mult)
            V(ts, R("BLN", 0, 16), R("BLK", 0, 16), -1.0, None, A.mult)
        V(ts, R("CSi", 0, 256), R("r15I", 0, 256), c1("colA"), None, A.mult)
        V(ts, c1("pk1"), c1("p16"), 8.0, 24.0, A.mult, A.add)
        V(tt, c1("pk2"), c1("pk1"), c1("p16"), A.mult)
        V(ts, R("PICK", 0, 1), c1("pk2"), 15.0, None, A.add)
        V(ts, R("DUE", 0, 16), R("duI", 0, 16), c1("p16"), 1024.0, A.add, A.add)
        V(ts, R("DUJ", 0, 16), R("duI", 0, 16), c1("p16"), 2048.0, A.add, A.add)
        V("memset", R("DM", 0, 2176), 1.0)
        V(ts, R("OWN", 0, 16), R("rI", 0, 16), c1("p16"), 1.0, A.is_equal, A.add)
        for q in range(16):
            e = 8 * (q + 1) * (q + 2)
            S(R("DM", e - 16, e), R("OWN", 0, 16), F.Copy)
        for q in range(16):
            s = 8 * q * (q + 1)
            S(R("DM", s, s + 1), c1("pz"), F.Copy)
        V(ts, c1("k15"), c1("p16"), -1.0, 15.0, A.mult, A.add)
        V(ts, R("RPR", 0, 128), R("dgI", 0, 128), 0.0, None, A.is_equal)
        V(ts, R("RPt", 0, 128), R("dgI", 0, 128), 0.0, 4096.0, A.is_equal, A.mult)
        V(ts, R("RPJ", 0, 128), R("dgI", 0, 128), -8.0, None, A.is_equal)
        V(tt, R("RPJ", 0, 128), R("RPJ", 0, 128), R("RPt", 0, 128), A.add)
        V(ts, R("RPN", 0, 128), R("dgI", 0, 128), -16.0, None, A.is_equal)
        V(ts, R("RPK", 0, 128), R("dgI", 0, 128), -24.0, None, A.is_equal)

    def dedupe(row, col, cw, eq, du, fl):
        items = []
        for q in range(16):
            s, n = 8 * q * (q + 1), 16 * (q + 1)
            items.append((R(eq, s, s + n), R(row, 0, n), cw(q), None, A.is_equal))
        for a in range(0, 16, 4):
            VM(ts, items[a:a + 4])
        V("tensor_tensor_scan", R(du, 0, 2176), R("DM", 0, 2176), R(eq, 0, 2176), 0.0, A.mult, A.max)
        V(ts, R(fl, 0, 16), ind(R(du, 0, 2176), R("PICK", 0, 1)), -1.0, None, A.add)

    def size(relu, out, in_):
        if relu:
            V(ts, out, in_, 0.0, None, A.max)
        else:
            S(out, in_, F.Abs)

    def keys(relu, K, n, m, d, a, con, coni, payload):
        if relu:
            P([(R(K, 0, n), R("ONB", 0, 128), R("C0", 0, n), True, False)] +
              [(R(K, k, n, 16), R(d, k, 2048, 16), R("BLN", 0, n // 16), False, False) for k in range(m)])
            P([(R(K, k, n, 16), R(a, k, 2048, 16), R("BL2", 0, n // 16), False, False) for k in range(m)] +
              [(R(K, 0, n), R("ONB", 0, 128), R(coni, 0, n), False, False)] +
              [(o, l, r, False, i == len(payload) - 1) for i, (o, l, r) in enumerate(payload)])
        else:
            P([(R(K, 0, n), R("ONB", 0, 128), R(con, 0, n), True, False)] + [(o, l, r, False, False) for o, l, r in payload])
            P([(R(K, k, n, 16), R(a, k, 2048, 16), R("BLK", 0, n // 16), False, k == m - 1) for k in range(m)])

    I16, IB, INB = R("IW", 4, 132), R("IB", 4, 132), R("INB", 4, 132)
    ISH = R("IW", 5, 133)
    for t in range(3):
        z = "z%d" % t
        P([(R("b0", 8 * h, 8 * h + 8), R(z, 128 * h, 128 * h + 128), R("W8", 0, 8), True, True) for h in (0, 1)])
        V(tc, R("ui", 0, 16), R("b0", 0, 16))
        V(ts, R("ui", 0, 16), R("ui", 0, 16), 4095, None, A.bitwise_and)
        V(tt, R("uu", 0, 16), R("ui", 0, 16), R("ui", 0, 16), A.mult)
        V(ts, R("UQ", 0, 16), R("ui", 0, 16), 2047, None, A.bitwise_and)
        V(ts, R("UQ", 16, 32), R("uu", 0, 16), 4, 2047, A.arith_shift_right, A.bitwise_and)
        V(ts, R("UQ", 32, 48), R("uu", 0, 16), 5, 1023, A.arith_shift_right, A.bitwise_and)
        V(tc, R("UH", 0, 48), R("UQ", 0, 48))
        P([(R("b0", 128, 256, 1, 48), R("UH", 0, 48), I16, True, True)])
        S(R("RLu", 0, 128, 1, 48), R("b0", 128, 256, 1, 48), F.Copy)
        P([(R("b0", 256 + 128 * h, 384 + 128 * h), R("PM_%d" % h, 0, 128, 1, 48), R("RLu", 0, 128, 1, 48), True, True) for h in (0, 1)])
        if t == 0:
            V(tc, R("em", 0, 256), R("b0", 256, 512))
        else:
            V(ts, R("em", 0, 256), R("b0", 256, 512), c1("Ac"), None, A.add)
        V(ts, R("em", 0, 256), R("em", 0, 256), 1023, None, A.bitwise_and)
        V(tc, R("emu", 0, 256), R("em", 0, 256))
        nz = opt["zv"][t]
        zx = "zx%d" % (t % 2)
        VM(tc, [(R(zx, m, 4096, 16), R(z, 0, 256)) for m in range(nz)])
        for m in range(nz, 16):
            S(R(zx, m, 4096, 16), R(z, 0, 256), F.Copy)
        V(tc, R("emh", 0, 256), R("emu", 0, 256))
        for h in (0, 1):
            H, K = "_%d" % h, "b%d" % (2 + h)
            ch = opt["gchunk"]
            w = 2048 // ch
            for c in range(ch):
                V(tt, R("DG" + H, w * c, w * c + w), ind(R("G", 0, 1024), R("emu", 128 * h + w // 16 * c, 128 * h + w // 16 * (c + 1))),
                  R(zx, 2048 * h + w * c, 2048 * h + w * c + w), A.subtract)
                size(opt["rg"][h], R("AG" + H, w * c, w * c + w), R("DG" + H, w * c, w * c + w))
            keys(opt["rg"][h], K, 128, 16, "DG" + H, "AG" + H, "CD", "CDi", [(R(K, 0, 128), R("emh", 128 * h, 128 * h + 128), I16)])
        if t == 0:
            load_names()
        for h in (0, 1):
            H, K = "_%d" % h, "b%d" % (2 + h)
            V("tensor_tensor_scan", R("km" + H, 0, 128), R("MMIN", 0, 128), R(K, 0, 128), 0.0, A.max, A.min)
            V(tc, R("ei" + H, 0, 8), R("km" + H, 15, 128, 16))
            V(ts, R("ej" + H, 0, 8), R("ei" + H, 0, 8), 1023, None, A.bitwise_and)
            V(tt, R("ME" + H, 0, 128), ind(R("ej" + H, 0, 8), R("OFFR", 0, 8)), R("MK", 0, 128), A.mult)
            P([(R("b7", 8 * h, 8 * h + 8), R("ME" + H, 0, 128), R("Q16", 0, 8), True, True)])
            V(tc, R("eu" + H, 0, 8), R("b7", 8 * h, 8 * h + 8))
            V(tc, R("Ju" + H, 0, 128), ind(R("I", 0, 1024), R("eu" + H, 0, 8)))
            V(tc, R("Jh", 128 * h, 128 * h + 128), R("Ju" + H, 0, 128))
            V(tc, R("e_rq", 8 * h, 8 * h + 8), R("eu" + H, 0, 8))
            P([(R("b7", 256 + 128 * h, 384 + 128 * h), R("ME" + H, 0, 128), I16, True, True)])
        if t == 0:
            late_constants()
            load_links()
        for h in (0, 1):
            H, K = "_%d" % h, "b%d" % (2 + h)
            lk = ind(R("L", 0, 2048), R("Ju" + H, 0, 128))
            xg = ind(R("xb", 0, 2048), R("Ju" + H, 0, 128))
            if opt["lv"][h]:
                V(tc, R("Lg" + H, 0, 2048), lk)
            else:
                S(R("Lg" + H, 0, 2048), lk, F.Copy)
            if opt["xv"][h]:
                V(tc, R("x" + H, 0, 2048), xg)
            else:
                S(R("x" + H, 0, 2048), xg, F.Copy)
            P([(R("b6", 128 * h, 128 * h + 128), R("SEL", 128 * k, 128 * k + 128), R("Lg" + H, k, 2048, 16), k == 0, k == 15) for k in range(16)])
            V(tc, R("nu" + H, 0, 128), R("b6", 128 * h, 128 * h + 128))
            yc = opt["ychunk"]
            w = 2048 // yc
            for c in range(yc):
                V(tt, R("Dy" + H, w * c, w * c + w), ind(R("xb", 0, 2048), R("nu" + H, w // 16 * c, w // 16 * (c + 1))), R("x" + H, w * c + 1, w * c + w + 1), A.subtract)
                size(opt["ry"][h], R("Ay" + H, w * c, w * c + w), R("Dy" + H, w * c, w * c + w))
            V("tensor_tensor_scan", R("mx" + H, 0, 2048), R("MR", 0, 2048), R("x" + H, 0, 2048), 0.0, A.mult, A.max)
        P([(R("b6", 256 + 128 * h, 384 + 128 * h), IB, R(z, 128 * h, 128 * h + 128), True, False) if a == 0 else
           (R("b6", 256 + 128 * h, 384 + 128 * h), IB, R("mx_%d" % h, 15, 2048, 16), False, True) for h in (0, 1) for a in (0, 1)])
        S(R("zt", 0, 256), R("b6", 256, 512), F.Copy, 127.75, 0.5)
        V(ts, R("zs%d" % t, 0, 256), R("zt", 0, 256), -128.0, None, A.add)
        add("g", "remote", [(t,)], [R("zs%d" % t, 0, 256)], [R("z%d" % (t + 1), 0, 256)], 300, 4000)
        S(R("Y", 0, 256), R("b7", 256, 512), F.Copy)
        P([(R("b7", 256, 512), R("BH", 0, 128), R("Y", 0, 256), True, True)])
        S(R("Er", 0, 256), R("b7", 256, 512), F.Copy)
        dedupe("Er", None, lambda q: R("e_rq", q, q + 1), "EQE", "DUPE", "fl")
        V(tt, R("of1", 0, 16), R("fl", 0, 16), R("DUE", 0, 16), A.mult)
        V(tt, R("of2", 0, 16), R("of1", 0, 16), R("e_rq", 0, 16), A.max)
        V(tc, R("oEu", 0, 16), R("of2", 0, 16))
        P([(R("b0", 256 + 128 * h, 384 + 128 * h), R("PQ_%d" % h, 0, 128, 1, 48), R("RLu", 0, 128, 1, 48), True, True) for h in (0, 1)])
        V(tc, R("vi", 0, 256), R("b0", 256, 512))
        V(ts, R("vi", 0, 256), R("vi", 0, 256), 2047, None, A.bitwise_and)
        S(R("Jf", 0, 256), R("Jh", 0, 256), F.Copy)
        VJ = R("b3", 256, 512)
        P([(R("b2", 256, 512), I16, R("Jh", 0, 256), True, True)])
        V(tt, VJ, R("vi", 0, 256), R("b2", 256, 512), A.subtract)
        for h in (0, 1):
            H, K = "_%d" % h, "b%d" % (2 + h)
            J = R("Jh", 128 * h, 128 * h + 128)
            keys(opt["ry"][h], K, 256, 15, "Dy" + H, "Ay" + H, "CS", "CSi", [(R(K, 0, 128), J, I16), (R(K, 128, 256), J, ISH)])
            V(tt, R("le" + H, 0, 128), R(K, 0, 128), R("THR", 0, 128), A.is_lt)
            V("tensor_tensor_scan", R("sm" + H, 0, 256), R("MMAX", 0, 256), R(K, 0, 256), 0.0, A.min, A.max)
            V("tensor_tensor_scan", R("cs" + H, 0, 128), R("MR", 0, 128), R("le" + H, 0, 128), 0.0, A.mult, A.add)
            V(tc, R("si" + H, 0, 16), R("sm" + H, 15, 256, 16))
            V(ts, R("QT" + H, 0, 8), R("cs" + H, 15, 128, 16), 11.5, None, A.is_gt)
            V(ts, R("sj" + H, 0, 16), R("si" + H, 0, 16), 2047, None, A.bitwise_and)
            V(ts, R("sj" + H, 16, 24), R("si" + H, 0, 8), 11, 15, A.arith_shift_right, A.bitwise_and)
            V(tc, R("QT" + H, 8, 32), R("sj" + H, 0, 24))
            P([(R("b7", 128, 256, 1, 32), R("QT" + H, 0, 32), I16, True, True)])
            S(R("RL", 128 * h, 128 * h + 128, 1, 32), R("b7", 128, 256, 1, 32), F.Copy)
        if t < 2:
            P([(R("b7", 16, 24), R("ONH", 0, 128), R("QT_0", 0, 8), True, False), (R("b7", 16, 24), R("ONH", 0, 128), R("QT_1", 0, 8), False, True)])
            V("tensor_reduce", c1("Ac"), R("b7", 16, 24), "X", A.add)
        RL = R("RL", 0, 256, 1, 32)
        P([(R("b6", 256, 512), R("RPJ", 0, 128, 1, 32), RL, True, True)])
        V(tt, R("mj", 0, 256), R("b6", 256, 512), R("MK", 0, 256), A.mult)
        S(R("RJh", 0, 256), R("b6", 256, 512), F.Copy)
        P([(R("b6", 0, 256), R("RPN", 0, 128, 1, 32), RL, True, True), (R("b6", 256, 512), R("RPK", 0, 128, 1, 32), RL, True, True)])
        V("tensor_tensor_scan", R("scj", 0, 256), R("MR", 0, 256), R("mj", 0, 256), 0.0, A.mult, A.add)
        JJ = R("scj", 15, 256, 16)
        if t < 2:
            V(ts, R("nr", 0, 16), JJ, 4095.5, None, A.is_lt)
            V(tt, R("og1", 0, 16), R("nr", 0, 16), R("DUE", 0, 16), A.mult)
            V(tt, R("og2", 0, 16), R("og1", 0, 16), R("of2", 0, 16), A.max)
            V(tc, R("oGu", 0, 16), R("og2", 0, 16))
            V(tc, ind(R("G", 0, 1280), R("oGu", 0, 16)), R(z, 0, 256))
        for h in (0, 1):
            H = "_%d" % h
            for c in range(4):
                B = "b%d" % (4 + c % 2)
                P([(R(B, 0, 512), IB, R("x" + H, 512 * c, 512 * c + 512), True, False),
                   (R(B, 0, 512), INB, R(zx, 2048 * h + 512 * c, 2048 * h + 512 * c + 512), False, True)])
                S(R("Af" + H, 512 * c, 512 * c + 512), R(B, 0, 512), F.Abs)
            P([(R("b1", 128 * h, 128 * h + 128), R("ZB", 15 - k, 143 - k), R("Af" + H, k, 2048, 16), k == 0, k == 15) for k in range(16)])
            V(ts, R("far", 128 * h, 128 * h + 128), R("b1", 128 * h, 128 * h + 128), R("tf", 1, 2), None, A.is_gt)
        P([(R("b1", 256, 512), R("RPR", 0, 128, 1, 32), RL, True, True)])
        V(tt, R("ch", 0, 256), R("b1", 256, 512), R("far", 0, 256), A.max)
        V(tt, R("tmp", 0, 256), R("ch", 0, 256), VJ, A.mult)
        V(tt, ind(R("I", 0, 1280), R("oEu", 0, 16)), R("tmp", 0, 256), R("Jf", 0, 256), A.add)
        if t == 2:
            dma("y", "yi", R("I", 0, 1024), 4096, "d8")
        dedupe("RJh", None, lambda q: R("scj", 16 * q + 15, 16 * q + 16), "EQJ", "DUPJ", "flJ")
        V(tt, R("oj1", 0, 16), R("flJ", 0, 16), R("DUJ", 0, 16), A.mult)
        V(tt, R("oj2", 0, 16), R("oj1", 0, 16), JJ, A.max)
        V(tt, R("oj3", 0, 16), R("oj2", 0, 16), R("DUJ", 0, 16), A.min)
        V(tc, R("oJu", 0, 16), R("oj3", 0, 16))
        S(R("Lold", 0, 256), ind(R("L", 0, 2304), R("oJu", 0, 16)), F.Copy)
        V(ts, R("mk", 0, 256), R("b6", 256, 512), c1("k15"), None, A.is_equal)
        V(tt, R("b6", 0, 256), R("b6", 0, 256), R("Lold", 0, 256), A.subtract)
        V(tt, R("t2", 0, 256), R("b6", 0, 256), R("mk", 0, 256), A.mult)
        V(tt, ind(R("L", 0, 2304), R("oJu", 0, 16)), R("t2", 0, 256), R("Lold", 0, 256), A.add)
    dma("s", "yz", R("z3", 0, 256), 512, "d9")
    dma("y", "yl", R("L", 0, 2048), 8192, "d10")
    return ops


def bank(r):
    return r[0] if r[0][0] == "b" and len(r[0]) == 2 else None


def edges(ops):
    touched, pre = {}, []
    for o in ops:
        e = {}
        for w, rs in ((True, o["writes"]), (False, o["reads"])):
            for r in rs:
                key = PLACE[r[0]][0] if False else r[0]
                for (j, s, sw) in touched.get(key, []):
                    same = ops[j]["q"] == o["q"]
                    if bank(r):
                        if not same:
                            e[j] = True
                        elif o["q"] == "t":
                            e.setdefault(j, False)
                        elif (w or sw) and clash(r, s):
                            e[j] = e.get(j, False) or bool(sw)
                    elif (w or sw) and clash(r, s):
                        need = True if not same else (sw or ops[j]["kind"] == "dma")
                        e[j] = e.get(j, False) or bool(need)
        pre.append(e)
        for w, rs in ((True, o["writes"]), (False, o["reads"])):
            for r in rs:
                touched.setdefault(r[0], []).append((o["i"], r, w))
    return pre


def label(o):
    r = (o["writes"] or o["reads"])[0]
    return o["q"] + r[0] + ("@%d" % r[1] if r[0][0] == "b" else "")


def schedule(ops, pre, bias):
    n = len(ops)
    succ = [[] for _ in range(n)]
    for i in range(n):
        for j in pre[i]:
            succ[j].append(i)
    rankv = [0.0] * n
    for i in range(n - 1, -1, -1):
        o = ops[i]
        b = 0.0
        for k in succ[i]:
            b = max(b, rankv[k] + (WAKE if pre[k][i] else 0.0))
        rankv[i] = b + o["cost"] + o["lat"]
    rankv = [rankv[i] + bias.get(label(ops[i]), 0.0) for i in range(n)]
    left = [len(pre[i]) for i in range(n)]
    ready = [0.0] * n
    free = {}
    avail = [i for i in range(n) if left[i] == 0]
    order, start = [], [0.0] * n
    while avail:
        best = None
        for i in avail:
            s = max(ready[i], free.get(ops[i]["q"], 0.0))
            key = (s, -rankv[i])
            if best is None or key < best[0]:
                best = (key, i)
        s0, q = best[0][0], ops[best[1]]["q"]
        i = best[1]
        for k in avail:
            if ops[k]["q"] == q and max(ready[k], free.get(q, 0.0)) <= s0 + 40 and rankv[k] > rankv[i]:
                i = k
        s = max(ready[i], free.get(q, 0.0))
        avail.remove(i)
        start[i] = s
        free[q] = s + ops[i]["cost"]
        order.append(i)
        fin = s + ops[i]["cost"] + ops[i]["lat"]
        for k in succ[i]:
            ready[k] = max(ready[k], fin + (WAKE if pre[k][i] else 0.0) if pre[k][i] else s)
            left[k] -= 1
            if left[k] == 0:
                avail.append(k)
    return order, start


URGE = """
vmk:-5 vDUPE:-1 vb6@0:-10 tb1@0:-16 vCS:31 sAy_1:-8 vONH:-16 vmx_0:-6 vI:-11 ve_rq:8 vp16i:9 szx1:-5 vx_1:13 vQ16:15 vUQ:-19 sAf_1:-8 vpk1:-21 vDUE:7 vDUPJ:-4 vmx_1:-5 vMMIN:-9 vBLK:8 tb6@256:25 szx0:-16 tb6@0:29 sAy_0:-4 vle_0:1 vch:6 tb5@0:4 vkm_0:17 vDy_1:-2 vk15:12 voEu:-19 sDM:2 vJh:4 vsi_0:5 vRPR:13 vp16:8 shki:-7 vRPN:13 vej_0:-5 vvi:4 vEQE:1 vL:6 gz1:2 yG:-15 vIW:-4 vsm_1:4 vpk3:4 yixi:3 vle_1:2 vOWN:-8 vsi_1:9 vsj_1:-1 yL:23 tb4@0:-5 gduI:7 vzs0:-3 sAG_1:1 vDG_0:-6 yxb:4 vzx0:-14 vZQ:-10 vemh:-1 vtf:-11 ylki:-12 vzs2:-11 gdI:2 tb7@16:-9 vej_1:2 vzx1:-1 vZB:1 vKM:2 sRL:3 vG:4 vMMAX:5 tb6@128:16 vDG_1:-5 vME_1:-4 vscj:-5 vUH:-10 gz3:-9 vBLN:-6 yz0:-4 vsj_0:1 vpk2:4 vPICK:2 sL:4 vnu_1:7 sJf:1 vONB:3 vEQJ:5 veu_0:9 voJu:-3 vx_0:-4 vW8:9 vINB:-1 voj3:2 vRPK:-3 vOFFR:8 gr15I:-1 vJu_0:-4 vCD:-6 voj2:-5 vt2:1 vDy_0:6 tb4@256:6 vIB:-6 tb1@128:6 vQT_1:-1 sx_0:3 tb7@128:3 grI:-7 sPQ_1:3 vTHR:-4 vDM:-1 sz3:-8 veu_1:-4 vfl:1 vdgA:-3 vuu:-1 vAc:5 vcs_1:-1 vME_0:-3 tb2@256:-10 szt:1 voj1:1 vmj:-1 vnr:-2 gdgI:3 sEr:6 vwf:-1 sLg_0:-3 vMK:3 gz2:3 gcI:3 sRLu:-5 sRJh:3 vzs1:-1 tb0@0:5 vog2:-3 sthi:-5 vkm_1:1 ggI:8 vof1:5 sAG_0:-1 tb7@8:-3 sLold:1
"""
OPT = {"gchunk": 1, "ychunk": 4, "lv": (0, 0), "xv": (0, 1), "zv": (0, 0, 0), "rg": (0, 0), "ry": (0, 0),
       "bias": {w.split(":")[0]: 500.0 * int(w.split(":")[1]) for w in URGE.split()}}
PLAN = {}


def rank_program(g, core, T, topo):
    rank = T.rank_of(core)
    if rank is None:
        return
    if "ops" not in PLAN:
        PLAN["ops"] = build(rank, OPT)
        PLAN["pre"] = edges(PLAN["ops"])
        PLAN["order"], PLAN["start"] = schedule(PLAN["ops"], PLAN["pre"], OPT["bias"])
    ops, pre = PLAN["ops"], PLAN["pre"]
    nxt = T.cores[(rank + 1) % len(T.cores)]
    home = T.cores[(rank + 2) % len(T.cores)]
    queue = {"v": g.vector, "s": g.scalar, "t": g.tensor, "g": g, "y": g.sync}
    qsem = {"v": "qv", "s": "qs", "t": "qt", "g": "qg"}
    count = {}
    seen = {q: {} for q in queue}
    done = {}

    def ap(r):
        if isinstance(r, IndOp):
            return ap(r[0]).indirect(ap(r[1]))
        name, off = PLACE[r[0]]
        a, b, st, p = r[1] + off, r[2] + off, r[3], r[4]
        t = T[name]
        if st == 1:
            return t[:, a:b] if p == 128 else t[0:p, a:b]
        return t[:, a:b:st]

    def arg(x):
        return ap(x) if isinstance(x, tuple) else x

    place = {i: n for n, i in enumerate(PLAN["order"])}
    for i in PLAN["order"]:
        o = ops[i]
        q, eng = o["q"], queue[o["q"]]
        known = seen[q]
        for j in sorted(pre[i], key=lambda j: -place[j]):
            if not pre[i][j]:
                continue
            sem, val, kn = done[j]
            if known.get(sem, 0) < val:
                eng.wait_ge(T.sem[sem], val)
                for k in kn:
                    known[k] = max(known.get(k, 0), kn[k])
                known[sem] = max(known.get(sem, 0), val)
        if o["kind"] == "dma":
            out, in_ = o["calls"][0]
            out = ap(out) if isinstance(out, tuple) else T[out][:]
            in_ = ap(in_) if isinstance(in_, tuple) else T[in_][:]
            eng.dma_start(out, in_).then_inc(T.sem[o["sem"]], 16)
            done[i] = (o["sem"], 16, dict(known))
            count[o["sem"]] = 16
            continue
        if o["kind"] == "remote":
            t = o["calls"][0][0]
            dst = nxt if t < 2 else home
            rid, pid, _e = topo.addr(dst)
            g.remote_dma(T["z%d" % (t + 1)][:], T["zs%d" % t][:], T.sem["arr%d" % (t + 1)], T.sem["loc"], pid, rid, topo.mask(core, dst))
            m = len(topo.engines(core, dst))
            src = T.cores[(rank - 1) % len(T.cores)] if t < 2 else T.cores[(rank - 2) % len(T.cores)]
            count["loc"] = count.get("loc", 0) + m
            done[i] = ("arr%d" % (t + 1), len(topo.engines(src, core)), {})
            continue
        sem = qsem[q]
        for c in o["calls"]:
            if o["kind"] == "matmul":
                ins = g.tensor.matmul(ap(c[0]), ap(c[1]), ap(c[2]), c[3], c[4])
            elif o["kind"] == "activation":
                kw = {}
                if c[3] is not None:
                    kw["bias"] = arg(c[3])
                if c[4] is not None:
                    kw["scale"] = arg(c[4])
                ins = g.scalar.activation(ap(c[0]), ap(c[1]), c[2], **kw)
            elif o["kind"] == "iota":
                ins = g.iota(ap(c[0]), c[1], c[2], c[3])
            else:
                x = [arg(y) for y in c]
                k = o["kind"]
                if k == "tensor_copy":
                    ins = g.vector.tensor_copy(*x)
                elif k == "tensor_scalar":
                    ins = g.vector.tensor_scalar(*x)
                elif k == "tensor_tensor":
                    ins = g.vector.tensor_tensor(*x)
                elif k == "tensor_tensor_scan":
                    ins = g.vector.tensor_tensor_scan(*x)
                elif k == "tensor_reduce":
                    ins = g.vector.tensor_reduce(x[0], x[1], AxisListType.X, x[3])
                else:
                    ins = g.vector.memset(*x)
            ins.then_inc(T.sem[sem], 1)
            count[sem] = count.get(sem, 0) + 1
        kn = dict(known)
        kn[sem] = count[sem]
        done[i] = (sem, count[sem], kn)
    for sem in sorted(count):
        g.wait_ge(T.sem[sem], count[sem])
